import numpy as np
import ml_dtypes


def mxq(x, axis, fmt="e4m3"):
    dtype, down = {"e4m3": (ml_dtypes.float8_e4m3fn, 7), "e5m2": (ml_dtypes.float8_e5m2, 14)}[fmt]
    v = np.moveaxis(np.asarray(x, np.float32).astype(ml_dtypes.bfloat16).astype(np.float64), axis, -1)
    blocks = v.reshape(v.shape[:-1] + (-1, 32))
    amax = np.abs(blocks).max(-1, keepdims=True)
    byte = np.maximum(np.where(amax > 0, np.frexp(amax)[1] - 1 + 127, 0) - down, 1)
    scale = np.exp2(byte - 127.0)
    codes = (blocks / scale).astype(np.float32).astype(dtype).astype(np.float64)
    return np.moveaxis((codes * scale).reshape(v.shape), -1, axis)


WIDE = False


def mx_kscale(k):
    if not WIDE:
        return np.ones(k)
    levels = np.array([10, -10, 5, -5, 0])
    if k % 512:
        return np.exp2(np.random.permutation(np.resize(levels, k // 32))).repeat(32)
    a = np.empty((k // 512, 16))
    for p in range(k // 512):
        a[p, :8] = np.random.permutation(np.resize(levels, 8))
        for g in range(8):
            far = levels[np.abs(levels - a[p, g]) >= 10]
            a[p, g + 8] = far[np.random.randint(len(far))]
    return np.exp2(a.ravel()).repeat(32)


def f64(x):
    return np.asarray(x).astype(np.float64)


E2M1 = np.array([0.0, 0.5, 1.0, 1.5, 2.0, 3.0, 4.0, 6.0, -0.0, -0.5, -1.0, -1.5, -2.0, -3.0, -4.0, -6.0])


def pack_weight(w, fmt):
    k, n = w.shape
    w = f64(np.asarray(w, np.float32).astype(ml_dtypes.bfloat16)).reshape(k // 32, 32, n)
    amax = np.abs(w).max(1)
    if fmt == "e4m3":
        byte = np.frexp(amax)[1] - 1 + 127 - 7
    else:
        mant, ex = np.frexp(amax / 6.0)
        byte = np.where(mant > 0.5, ex, ex - 1) + 127
    byte = np.clip(np.where(amax > 0, byte, 1), 1, 254)
    scaled = (w * np.exp2(127.0 - byte)[:, None, :]).reshape(k, n).astype(np.float32)
    by_word = np.ascontiguousarray(scaled.reshape(k // 512, 128, 4, n).transpose(0, 1, 3, 2))
    if fmt == "e4m3":
        words = by_word.astype(ml_dtypes.float8_e4m3fn).view(np.uint8)
    else:
        c = by_word.astype(ml_dtypes.float4_e2m1fn).view(np.uint8) & 0xF
        words = (c[..., 0::2] | (c[..., 1::2] << 4)).reshape(k // 512, 128, 2 * n)
    return np.ascontiguousarray(words), np.ascontiguousarray(byte.astype(np.uint8).reshape(k // 512, 16, n))


def unpack_weight(words, scales, fmt):
    g, _, n = scales.shape
    words = np.ascontiguousarray(words).reshape(g, 128, n, -1)
    if fmt == "e4m3":
        vals = words.view(ml_dtypes.float8_e4m3fn).astype(np.float64)
    else:
        nib = np.empty((g, 128, n, 4), np.uint8)
        nib[..., 0::2] = words & 0xF
        nib[..., 1::2] = words >> 4
        vals = E2M1[nib]
    vals = vals * np.repeat(np.exp2(scales.astype(np.float64) - 127.0), 8, axis=1)[..., None]
    return vals.transpose(0, 1, 3, 2).reshape(g * 512, n)


K, M, T = 1024, 1536, 512


def setup_inputs():
    n = np.random.standard_normal
    s = mx_kscale(K)[:, None]
    p_w4 = pack_weight(n((K, M)) / np.sqrt(K) / s ** 2, "e2m1")
    p_w8 = pack_weight(n((K, M)) / np.sqrt(K) / s, "e4m3")
    return {
        "x": (n((K, T)) * s).astype(np.float32),
        "w4_words": p_w4[0],
        "w4_scales": p_w4[1],
        "w8_words": p_w8[0],
        "w8_scales": p_w8[1],
    }


def reference(x, w4_words, w4_scales, w8_words, w8_scales):
    xa_, xb_ = mxq(f64(x) ** 2, 0, "e4m3"), mxq(f64(x), 0, "e4m3")
    w4_ = unpack_weight(w4_words, w4_scales, "e2m1")
    w8_ = unpack_weight(w8_words, w8_scales, "e4m3")
    y = w4_.T @ xa_ + w8_.T @ xb_
    return y

@@ -1,0 +1,210 @@
+from contextlib import ExitStack
+
+import concourse.mybir as mybir
+
+K, M, T = 1024, 1536, 512
+FLOPS = 2 * 2 * K * M * T
+
+F32 = mybir.dt.float32
+BF16 = mybir.dt.bfloat16
+I32 = mybir.dt.int32
+U32 = mybir.dt.uint32
+U8 = mybir.dt.uint8
+FP8X4 = mybir.dt.float8_e4m3fn_x4
+FP4X4 = mybir.dt.float4_e2m1fn_x4
+SQUARE = mybir.ActivationFunctionType.Square
+
+P = 128
+PACK = 4
+K_PASS = P * PACK
+PASSES = K // K_PASS
+TILES = M // P
+BANKS = 8
+HALF = T // 2
+W8_PLANE = 4
+RUN = 4
+LAG = 4
+
+
+def tile_mix_feat_fm_quad_none_kernel(tc, x, w4_words, w4_scales, w8_words, w8_scales, out):
+    nc = tc.nc
+    with ExitStack() as ctx:
+        keep = ctx.enter_context(tc.tile_pool(name="keep", bufs=1))
+        stage = ctx.enter_context(tc.tile_pool(name="stage", bufs=TILES + 1))
+        psum = ctx.enter_context(tc.psum_pool(name="psum", bufs=BANKS))
+        ctx.enter_context(tc.manual_schedule())
+
+        s8 = keep.tile([P, PASSES * M], U8, name="s8", align_bytes=64)
+        s4 = keep.tile([P, PASSES * M], U8, name="s4", align_bytes=64)
+        nc.vector.memset(s8[:].bitcast(I32), 0)
+        nc.vector.memset(s4[:].bitcast(I32), 0)
+
+        warm_in = keep.tile([P, 1], F32, name="warm_in")
+        warm_out = keep.tile([P, 1], F32, name="warm_out")
+        nc.gpsimd.memset(warm_in[:], 0.0)
+        nc.scalar.activation(out=warm_out[:], in_=warm_in[:], func=SQUARE)
+
+        raw = {}
+
+        def load_x(a, h):
+            t = keep.tile([P, PACK, HALF], F32, name="raw_%d_%d" % (a, h), align_bytes=64)
+            rows = x[a * K_PASS : (a + 1) * K_PASS, h * HALF : (h + 1) * HALF]
+            nc.sync.dma_start(out=t[:], in_=rows.rearrange("(p j) w -> p j w", j=PACK))
+            raw[a, h] = t
+
+        def load_scales(plane, scales, first):
+            for r in range(4):
+                dst = plane[first + r : P : 32, :].bitcast(I32).rearrange("q (a n) -> q a n", a=PASSES)
+                src = scales[:, r:16:4, :].rearrange("a q n -> q a n").bitcast(I32)
+                nc.sync.dma_start(out=dst, in_=src)
+
+        w8 = {}
+        w4 = {}
+
+        def load_w8(passes, lo, hi):
+            n = (hi - lo) * P
+            t = keep.tile([P, len(passes) * n], U32, name="w8_%d_%d" % (passes[0], lo), align_bytes=64)
+            src = w8_words[passes[0] : passes[-1] + 1].rearrange("a p n i -> p a (n i)")
+            nc.sync.dma_start(
+                out=t[:].bitcast(I32).rearrange("p (a n) -> p a n", a=len(passes)),
+                in_=src[:, :, PACK * lo * P : PACK * hi * P].bitcast(I32),
+            )
+            for i, a in enumerate(passes):
+                for m in range(lo, hi):
+                    c = i * n + (m - lo) * P
+                    w8[a, m] = t[:, c : c + P]
+
+        def load_w4(passes, lo, hi):
+            n = (hi - lo) * 2 * P
+            t = keep.tile([P, len(passes) * n], U8, name="w4_%d_%d" % (passes[0], lo), align_bytes=64)
+            src = w4_words[passes[0] : passes[-1] + 1].rearrange("a p b -> p a b")
+            nc.sync.dma_start(
+                out=t[:].bitcast(I32).rearrange("p (a n) -> p a n", a=len(passes)),
+                in_=src[:, :, 2 * lo * P : 2 * hi * P].bitcast(I32),
+            )
+            for i, a in enumerate(passes):
+                for m in range(lo, hi):
+                    c = i * n + (m - lo) * 2 * P
+                    w4[a, m] = t[:, c : c + 2 * P]
+
+        load_x(0, 0)
+        load_scales(s8, w8_scales, W8_PLANE)
+        load_w8([0], 0, BANKS // 2)
+        load_x(0, 1)
+        load_w8([0], BANKS // 2, BANKS)
+        load_x(1, 0)
+        load_scales(s4, w4_scales, 0)
+        load_w4([0], 0, BANKS)
+        load_x(1, 1)
+        load_w8([1], 0, BANKS)
+        load_w4([1], 0, BANKS)
+        load_w8([0, 1], BANKS, TILES)
+        load_w4([0, 1], BANKS, TILES)
+
+        codes = {}
+        planes = {}
+        for name in ("sq", "lin"):
+            for a in range(PASSES):
+                codes[name, a] = keep.tile([P, T], U32, name="codes_%s_%d" % (name, a), align_bytes=64)
+                planes[name, a] = keep.tile([P, T], U8, name="plane_%s_%d" % (name, a), align_bytes=64)
+
+        grouped = {}
+
+        def group(name, a, h):
+            g = keep.tile([P, HALF, PACK], BF16, name="g_%s_%d_%d" % (name, a, h), align_bytes=64)
+            dst = g[:].rearrange("p (c i) j -> p c j i", i=RUN)
+            src = raw[a, h][:].rearrange("p j (c i) -> p c j i", i=RUN)
+            if name == "sq":
+                nc.scalar.activation(out=dst, in_=src, func=SQUARE)
+            else:
+                nc.vector.tensor_copy(out=dst, in_=src)
+            grouped[name, a, h] = g
+
+        def quantize(name, a, h):
+            cols = slice(h * HALF, (h + 1) * HALF)
+            nc.vector.quantize_mx(
+                out=codes[name, a][:, cols].bitcast(FP8X4),
+                scales=planes[name, a][:, cols],
+                in_=grouped[name, a, h][:].rearrange("p w j -> p (w j)"),
+            )
+
+        for a in range(PASSES):
+            for h in range(2):
+                group("sq", a, h)
+        group("lin", 0, 0)
+        quantize("lin", 0, 0)
+        quantize("sq", 0, 0)
+        group("lin", 0, 1)
+        quantize("lin", 0, 1)
+        quantize("sq", 0, 1)
+        group("lin", 1, 0)
+        quantize("lin", 1, 0)
+        quantize("sq", 1, 0)
+        group("lin", 1, 1)
+        quantize("lin", 1, 1)
+        quantize("sq", 1, 1)
+
+        acc = {}
+
+        def linear_pass(a, m, cols, start):
+            sc = slice(a * M + m * P, a * M + (m + 1) * P)
+            nc.tensor.matmul_mx(
+                out=acc[m][:, cols],
+                lhsT=w8[a, m].bitcast(FP8X4),
+                lhsT_scale=s8[W8_PLANE:, sc],
+                rhs=codes["lin", a][:, cols].bitcast(FP8X4),
+                rhs_scale=planes["lin", a][:, cols],
+                start=start,
+                stop=False,
+            )
+
+        def square_pass(a, m, stop, cols=slice(0, T)):
+            sc = slice(a * M + m * P, a * M + (m + 1) * P)
+            nc.tensor.matmul_mx(
+                out=acc[m][:, cols],
+                lhsT=w4[a, m].bitcast(FP4X4),
+                lhsT_scale=s4[:, sc],
+                rhs=codes["sq", a][:, cols].bitcast(FP8X4),
+                rhs_scale=planes["sq", a][:, cols],
+                start=False,
+                stop=stop,
+            )
+
+        def drain(m, cols=slice(0, T)):
+            res = stage.tile([P, T], F32, name="res")
+            if (m + (cols.stop < T)) % 2 == 0:
+                nc.scalar.copy(out=res[:, cols], in_=acc[m][:, cols])
+            else:
+                nc.vector.tensor_copy(out=res[:, cols], in_=acc[m][:, cols])
+            nc.sync.dma_start(out=out[m * P : (m + 1) * P, cols], in_=res[:, cols])
+
+        whole = slice(0, T)
+        for m in range(BANKS):
+            acc[m] = psum.tile([P, T], F32, name="acc")
+            linear_pass(0, m, slice(0, HALF), True)
+        for m in range(BANKS):
+            linear_pass(0, m, slice(HALF, T), False)
+        for m in range(BANKS):
+            square_pass(0, m, False)
+        for step in range(BANKS + LAG):
+            if step < BANKS:
+                linear_pass(1, step, whole, False)
+            if step >= LAG:
+                square_pass(1, step - LAG, True)
+                drain(step - LAG)
+        for m in range(BANKS, TILES - 1):
+            acc[m] = psum.tile([P, T], F32, name="acc")
+            linear_pass(0, m, whole, True)
+            square_pass(0, m, False)
+            linear_pass(1, m, whole, False)
+            square_pass(1, m, True)
+            drain(m)
+        m = TILES - 1
+        for h in range(2):
+            acc[m] = psum.tile([P, T], F32, name="acc")
+            cols = slice(h * HALF, (h + 1) * HALF)
+            for a in range(PASSES):
+                linear_pass(a, m, cols, a == 0)
+                square_pass(a, m, False, slice(cols.start, cols.start + P))
+                square_pass(a, m, a == PASSES - 1, slice(cols.start + P, cols.stop))
+            drain(m, cols)

@@ -21,7 +21,7 @@ PASSES = K // K_PASS
 TILES = M // P
 BANKS = 8
 HALF = T // 2
-W8_PLANE = 4
+QUARTER = M // 4
 RUN = 4
 LAG = 4
 
@@ -34,14 +34,14 @@ def tile_mix_feat_fm_quad_none_kernel(tc, x, w4_words, w4_scales, w8_words, w8_s
         psum = ctx.enter_context(tc.psum_pool(name="psum", bufs=BANKS))
         ctx.enter_context(tc.manual_schedule())
 
-        s8 = keep.tile([P, PASSES * M], U8, name="s8", align_bytes=64)
+        s8 = keep.tile([P, PASSES * QUARTER], U8, name="s8", align_bytes=64)
         s4 = keep.tile([P, PASSES * M], U8, name="s4", align_bytes=64)
         nc.vector.memset(s8[:].bitcast(I32), 0)
-        nc.vector.memset(s4[:].bitcast(I32), 0)
+        nc.gpsimd.memset(s4[:].bitcast(I32), 0)
 
         warm_in = keep.tile([P, 1], F32, name="warm_in")
         warm_out = keep.tile([P, 1], F32, name="warm_out")
-        nc.gpsimd.memset(warm_in[:], 0.0)
+        nc.vector.memset(warm_in[:], 0.0)
         nc.scalar.activation(out=warm_out[:], in_=warm_in[:], func=SQUARE)
 
         raw = {}
@@ -52,10 +52,15 @@ def tile_mix_feat_fm_quad_none_kernel(tc, x, w4_words, w4_scales, w8_words, w8_s
             nc.sync.dma_start(out=t[:], in_=rows.rearrange("(p j) w -> p j w", j=PACK))
             raw[a, h] = t
 
-        def load_scales(plane, scales, first):
-            for r in range(4):
-                dst = plane[first + r : P : 32, :].bitcast(I32).rearrange("q (a n) -> q a n", a=PASSES)
-                src = scales[:, r:16:4, :].rearrange("a q n -> q a n").bitcast(I32)
+        for r in range(4):
+            dst = s4[r:P:32, :].bitcast(I32).rearrange("q (a n) -> q a n", a=PASSES)
+            src = w4_scales[:, r:16:4, :].rearrange("a q n -> q a n").bitcast(I32)
+            nc.gpsimd.dma_start(out=dst, in_=src)
+
+        def load_w8_scales(a):
+            for q in range(4):
+                dst = s8[32 * q : 32 * q + 16, a * QUARTER : (a + 1) * QUARTER].bitcast(I32)
+                src = w8_scales[a, 4 * q : 4 * q + 4, :].rearrange("r (c n) -> c r n", c=4).bitcast(I32)
                 nc.sync.dma_start(out=dst, in_=src)
 
         w8 = {}
@@ -88,14 +93,14 @@ def tile_mix_feat_fm_quad_none_kernel(tc, x, w4_words, w4_scales, w8_words, w8_s
                     w4[a, m] = t[:, c : c + 2 * P]
 
         load_x(0, 0)
-        load_scales(s8, w8_scales, W8_PLANE)
+        load_w8_scales(0)
         load_w8([0], 0, BANKS // 2)
         load_x(0, 1)
         load_w8([0], BANKS // 2, BANKS)
         load_x(1, 0)
-        load_scales(s4, w4_scales, 0)
         load_w4([0], 0, BANKS)
         load_x(1, 1)
+        load_w8_scales(1)
         load_w8([1], 0, BANKS)
         load_w4([1], 0, BANKS)
         load_w8([0, 1], BANKS, TILES)
@@ -147,11 +152,12 @@ def tile_mix_feat_fm_quad_none_kernel(tc, x, w4_words, w4_scales, w8_words, w8_s
         acc = {}
 
         def linear_pass(a, m, cols, start):
-            sc = slice(a * M + m * P, a * M + (m + 1) * P)
+            c, first = divmod(m * P, QUARTER)
+            sc = slice(a * QUARTER + first, a * QUARTER + first + P)
             nc.tensor.matmul_mx(
                 out=acc[m][:, cols],
                 lhsT=w8[a, m].bitcast(FP8X4),
-                lhsT_scale=s8[W8_PLANE:, sc],
+                lhsT_scale=s8[4 * c :, sc],
                 rhs=codes["lin", a][:, cols].bitcast(FP8X4),
                 rhs_scale=planes["lin", a][:, cols],
                 start=start,

@@ -23,7 +23,6 @@ BANKS = 8
 HALF = T // 2
 QUARTER = M // 4
 RUN = 4
-LAG = 4
 
 
 def tile_mix_feat_fm_quad_none_kernel(tc, x, w4_words, w4_scales, w8_words, w8_scales, out):
@@ -37,12 +36,12 @@ def tile_mix_feat_fm_quad_none_kernel(tc, x, w4_words, w4_scales, w8_words, w8_s
         s8 = keep.tile([P, PASSES * QUARTER], U8, name="s8", align_bytes=64)
         s4 = keep.tile([P, PASSES * M], U8, name="s4", align_bytes=64)
         nc.vector.memset(s8[:].bitcast(I32), 0)
-        nc.gpsimd.memset(s4[:].bitcast(I32), 0)
 
         warm_in = keep.tile([P, 1], F32, name="warm_in")
         warm_out = keep.tile([P, 1], F32, name="warm_out")
         nc.vector.memset(warm_in[:], 0.0)
         nc.scalar.activation(out=warm_out[:], in_=warm_in[:], func=SQUARE)
+        nc.vector.memset(s4[:].bitcast(I32), 0)
 
         raw = {}
 
@@ -52,10 +51,11 @@ def tile_mix_feat_fm_quad_none_kernel(tc, x, w4_words, w4_scales, w8_words, w8_s
             nc.sync.dma_start(out=t[:], in_=rows.rearrange("(p j) w -> p j w", j=PACK))
             raw[a, h] = t
 
-        for r in range(4):
-            dst = s4[r:P:32, :].bitcast(I32).rearrange("q (a n) -> q a n", a=PASSES)
-            src = w4_scales[:, r:16:4, :].rearrange("a q n -> q a n").bitcast(I32)
-            nc.gpsimd.dma_start(out=dst, in_=src)
+        def load_w4_scales():
+            for r in range(4):
+                dst = s4[r:P:32, :].bitcast(I32).rearrange("q (a n) -> q a n", a=PASSES)
+                src = w4_scales[:, r:16:4, :].rearrange("a q n -> q a n").bitcast(I32)
+                nc.sync.dma_start(out=dst, in_=src)
 
         def load_w8_scales(a):
             for q in range(4):
@@ -97,12 +97,14 @@ def tile_mix_feat_fm_quad_none_kernel(tc, x, w4_words, w4_scales, w8_words, w8_s
         load_w8([0], 0, BANKS // 2)
         load_x(0, 1)
         load_w8([0], BANKS // 2, BANKS)
-        load_x(1, 0)
+        load_w4_scales()
         load_w4([0], 0, BANKS)
+        load_x(1, 0)
         load_x(1, 1)
         load_w8_scales(1)
-        load_w8([1], 0, BANKS)
+        load_w8([1], 0, BANKS // 2)
         load_w4([1], 0, BANKS)
+        load_w8([1], BANKS // 2, BANKS)
         load_w8([0, 1], BANKS, TILES)
         load_w4([0, 1], BANKS, TILES)
 
@@ -144,9 +146,9 @@ def tile_mix_feat_fm_quad_none_kernel(tc, x, w4_words, w4_scales, w8_words, w8_s
         quantize("sq", 0, 1)
         group("lin", 1, 0)
         quantize("lin", 1, 0)
-        quantize("sq", 1, 0)
         group("lin", 1, 1)
         quantize("lin", 1, 1)
+        quantize("sq", 1, 0)
         quantize("sq", 1, 1)
 
         acc = {}
@@ -192,12 +194,12 @@ def tile_mix_feat_fm_quad_none_kernel(tc, x, w4_words, w4_scales, w8_words, w8_s
             linear_pass(0, m, slice(HALF, T), False)
         for m in range(BANKS):
             square_pass(0, m, False)
-        for step in range(BANKS + LAG):
-            if step < BANKS:
-                linear_pass(1, step, whole, False)
-            if step >= LAG:
-                square_pass(1, step - LAG, True)
-                drain(step - LAG)
+        for lo in (0, BANKS // 2):
+            for m in range(lo, lo + BANKS // 2):
+                linear_pass(1, m, whole, False)
+            for m in range(lo, lo + BANKS // 2):
+                square_pass(1, m, True)
+                drain(m)
         for m in range(BANKS, TILES - 1):
             acc[m] = psum.tile([P, T], F32, name="acc")
             linear_pass(0, m, whole, True)

@@ -45,11 +45,12 @@ def tile_mix_feat_fm_quad_none_kernel(tc, x, w4_words, w4_scales, w8_words, w8_s
 
         raw = {}
 
-        def load_x(a, h):
-            t = keep.tile([P, PACK, HALF], F32, name="raw_%d_%d" % (a, h), align_bytes=64)
-            rows = x[a * K_PASS : (a + 1) * K_PASS, h * HALF : (h + 1) * HALF]
+        def load_x(a, halves):
+            t = keep.tile([P, PACK, len(halves) * HALF], F32, name="raw_%d_%d" % (a, halves[0]), align_bytes=64)
+            rows = x[a * K_PASS : (a + 1) * K_PASS, halves[0] * HALF : (halves[-1] + 1) * HALF]
             nc.sync.dma_start(out=t[:], in_=rows.rearrange("(p j) w -> p j w", j=PACK))
-            raw[a, h] = t
+            for i, h in enumerate(halves):
+                raw[a, h] = t[:, :, i * HALF : (i + 1) * HALF]
 
         def load_w4_scales():
             for r in range(4):
@@ -92,15 +93,13 @@ def tile_mix_feat_fm_quad_none_kernel(tc, x, w4_words, w4_scales, w8_words, w8_s
                     c = i * n + (m - lo) * 2 * P
                     w4[a, m] = t[:, c : c + 2 * P]
 
-        load_x(0, 0)
+        load_x(0, [0, 1])
         load_w8_scales(0)
-        load_w8([0], 0, BANKS // 2)
-        load_x(0, 1)
-        load_w8([0], BANKS // 2, BANKS)
+        load_w8([0], 0, BANKS)
+        load_x(1, [0])
         load_w4_scales()
         load_w4([0], 0, BANKS)
-        load_x(1, 0)
-        load_x(1, 1)
+        load_x(1, [1])
         load_w8_scales(1)
         load_w8([1], 0, BANKS // 2)
         load_w4([1], 0, BANKS)
@@ -120,7 +119,7 @@ def tile_mix_feat_fm_quad_none_kernel(tc, x, w4_words, w4_scales, w8_words, w8_s
         def group(name, a, h):
             g = keep.tile([P, HALF, PACK], BF16, name="g_%s_%d_%d" % (name, a, h), align_bytes=64)
             dst = g[:].rearrange("p (c i) j -> p c j i", i=RUN)
-            src = raw[a, h][:].rearrange("p j (c i) -> p c j i", i=RUN)
+            src = raw[a, h].rearrange("p j (c i) -> p c j i", i=RUN)
             if name == "sq":
                 nc.scalar.activation(out=dst, in_=src, func=SQUARE)
             else:
@@ -138,18 +137,15 @@ def tile_mix_feat_fm_quad_none_kernel(tc, x, w4_words, w4_scales, w8_words, w8_s
         for a in range(PASSES):
             for h in range(2):
                 group("sq", a, h)
-        group("lin", 0, 0)
-        quantize("lin", 0, 0)
-        quantize("sq", 0, 0)
-        group("lin", 0, 1)
-        quantize("lin", 0, 1)
-        quantize("sq", 0, 1)
-        group("lin", 1, 0)
-        quantize("lin", 1, 0)
-        group("lin", 1, 1)
-        quantize("lin", 1, 1)
-        quantize("sq", 1, 0)
-        quantize("sq", 1, 1)
+        for h in range(2):
+            group("lin", 0, h)
+            quantize("lin", 0, h)
+        for h in range(2):
+            quantize("sq", 0, h)
+        for h in range(2):
+            group("lin", 1, h)
+            quantize("lin", 1, h)
+            quantize("sq", 1, h)
 
         acc = {}
 

@@ -37,10 +37,6 @@ def tile_mix_feat_fm_quad_none_kernel(tc, x, w4_words, w4_scales, w8_words, w8_s
         s4 = keep.tile([P, PASSES * M], U8, name="s4", align_bytes=64)
         nc.vector.memset(s8[:].bitcast(I32), 0)
 
-        warm_in = keep.tile([P, 1], F32, name="warm_in")
-        warm_out = keep.tile([P, 1], F32, name="warm_out")
-        nc.vector.memset(warm_in[:], 0.0)
-        nc.scalar.activation(out=warm_out[:], in_=warm_in[:], func=SQUARE)
         nc.vector.memset(s4[:].bitcast(I32), 0)
 
         raw = {}

@@ -21,43 +21,36 @@ PASSES = K // K_PASS
 TILES = M // P
 BANKS = 8
 HALF = T // 2
-QUARTER = M // 4
 RUN = 4
+SHIFT = 4
+FIRST = 8
 
 
 def tile_mix_feat_fm_quad_none_kernel(tc, x, w4_words, w4_scales, w8_words, w8_scales, out):
     nc = tc.nc
     with ExitStack() as ctx:
         keep = ctx.enter_context(tc.tile_pool(name="keep", bufs=1))
-        stage = ctx.enter_context(tc.tile_pool(name="stage", bufs=TILES + 1))
+        stage = ctx.enter_context(tc.tile_pool(name="stage", bufs=TILES + 2))
         psum = ctx.enter_context(tc.psum_pool(name="psum", bufs=BANKS))
         ctx.enter_context(tc.manual_schedule())
 
-        s8 = keep.tile([P, PASSES * QUARTER], U8, name="s8", align_bytes=64)
+        s8 = keep.tile([P, PASSES * M], U8, name="s8", align_bytes=64)
         s4 = keep.tile([P, PASSES * M], U8, name="s4", align_bytes=64)
         nc.vector.memset(s8[:].bitcast(I32), 0)
-
         nc.vector.memset(s4[:].bitcast(I32), 0)
 
         raw = {}
 
-        def load_x(a, halves):
-            t = keep.tile([P, PACK, len(halves) * HALF], F32, name="raw_%d_%d" % (a, halves[0]), align_bytes=64)
-            rows = x[a * K_PASS : (a + 1) * K_PASS, halves[0] * HALF : (halves[-1] + 1) * HALF]
+        def load_x(a, h):
+            t = keep.tile([P, PACK, HALF], F32, name="raw_%d_%d" % (a, h), align_bytes=64)
+            rows = x[a * K_PASS : (a + 1) * K_PASS, h * HALF : (h + 1) * HALF]
             nc.sync.dma_start(out=t[:], in_=rows.rearrange("(p j) w -> p j w", j=PACK))
-            for i, h in enumerate(halves):
-                raw[a, h] = t[:, :, i * HALF : (i + 1) * HALF]
+            raw[a, h] = t
 
-        def load_w4_scales():
+        def load_scales(plane, scales, shift):
             for r in range(4):
-                dst = s4[r:P:32, :].bitcast(I32).rearrange("q (a n) -> q a n", a=PASSES)
-                src = w4_scales[:, r:16:4, :].rearrange("a q n -> q a n").bitcast(I32)
-                nc.sync.dma_start(out=dst, in_=src)
-
-        def load_w8_scales(a):
-            for q in range(4):
-                dst = s8[32 * q : 32 * q + 16, a * QUARTER : (a + 1) * QUARTER].bitcast(I32)
-                src = w8_scales[a, 4 * q : 4 * q + 4, :].rearrange("r (c n) -> c r n", c=4).bitcast(I32)
+                dst = plane[shift + r : P : 32, :].bitcast(I32).rearrange("q (a n) -> q a n", a=PASSES)
+                src = scales[:, r:16:4, :].rearrange("a q n -> q a n").bitcast(I32)
                 nc.sync.dma_start(out=dst, in_=src)
 
         w8 = {}
@@ -89,20 +82,6 @@ def tile_mix_feat_fm_quad_none_kernel(tc, x, w4_words, w4_scales, w8_words, w8_s
                     c = i * n + (m - lo) * 2 * P
                     w4[a, m] = t[:, c : c + 2 * P]
 
-        load_x(0, [0, 1])
-        load_w8_scales(0)
-        load_w8([0], 0, BANKS)
-        load_x(1, [0])
-        load_w4_scales()
-        load_w4([0], 0, BANKS)
-        load_x(1, [1])
-        load_w8_scales(1)
-        load_w8([1], 0, BANKS // 2)
-        load_w4([1], 0, BANKS)
-        load_w8([1], BANKS // 2, BANKS)
-        load_w8([0, 1], BANKS, TILES)
-        load_w4([0, 1], BANKS, TILES)
-
         codes = {}
         planes = {}
         for name in ("sq", "lin"):
@@ -112,99 +91,133 @@ def tile_mix_feat_fm_quad_none_kernel(tc, x, w4_words, w4_scales, w8_words, w8_s
 
         grouped = {}
 
-        def group(name, a, h):
-            g = keep.tile([P, HALF, PACK], BF16, name="g_%s_%d_%d" % (name, a, h), align_bytes=64)
+        def group(name, a, h, lo=0, hi=HALF):
+            g = keep.tile([P, hi - lo, PACK], BF16, name="g_%s_%d_%d_%d" % (name, a, h, lo), align_bytes=64)
             dst = g[:].rearrange("p (c i) j -> p c j i", i=RUN)
-            src = raw[a, h].rearrange("p j (c i) -> p c j i", i=RUN)
+            src = raw[a, h][:, :, lo:hi].rearrange("p j (c i) -> p c j i", i=RUN)
             if name == "sq":
                 nc.scalar.activation(out=dst, in_=src, func=SQUARE)
             else:
                 nc.vector.tensor_copy(out=dst, in_=src)
-            grouped[name, a, h] = g
+            grouped[name, a, h, lo] = g
 
-        def quantize(name, a, h):
-            cols = slice(h * HALF, (h + 1) * HALF)
+        def quantize(name, a, h, lo=0, hi=HALF):
+            cols = slice(h * HALF + lo, h * HALF + hi)
             nc.vector.quantize_mx(
                 out=codes[name, a][:, cols].bitcast(FP8X4),
                 scales=planes[name, a][:, cols],
-                in_=grouped[name, a, h][:].rearrange("p w j -> p (w j)"),
+                in_=grouped[name, a, h, lo][:].rearrange("p w j -> p (w j)"),
             )
 
-        for a in range(PASSES):
-            for h in range(2):
-                group("sq", a, h)
-        for h in range(2):
-            group("lin", 0, h)
-            quantize("lin", 0, h)
-        for h in range(2):
-            quantize("sq", 0, h)
-        for h in range(2):
-            group("lin", 1, h)
-            quantize("lin", 1, h)
-            quantize("sq", 1, h)
+        def linear_operand(a, h):
+            for lo in (0, P):
+                group("lin", a, h, lo, lo + P)
+            for lo in (0, P):
+                quantize("lin", a, h, lo, lo + P)
 
-        acc = {}
-
-        def linear_pass(a, m, cols, start):
-            c, first = divmod(m * P, QUARTER)
-            sc = slice(a * QUARTER + first, a * QUARTER + first + P)
-            nc.tensor.matmul_mx(
-                out=acc[m][:, cols],
-                lhsT=w8[a, m].bitcast(FP8X4),
-                lhsT_scale=s8[4 * c :, sc],
-                rhs=codes["lin", a][:, cols].bitcast(FP8X4),
-                rhs_scale=planes["lin", a][:, cols],
-                start=start,
-                stop=False,
-            )
-
-        def square_pass(a, m, stop, cols=slice(0, T)):
+        def multiply(name, a, m, cols, dst, start=False, stop=False):
             sc = slice(a * M + m * P, a * M + (m + 1) * P)
+            if name == "sq":
+                weights, weight_scales = w4[a, m].bitcast(FP4X4), s4[:, sc]
+            else:
+                weights, weight_scales = w8[a, m].bitcast(FP8X4), s8[SHIFT:, sc]
             nc.tensor.matmul_mx(
-                out=acc[m][:, cols],
-                lhsT=w4[a, m].bitcast(FP4X4),
-                lhsT_scale=s4[:, sc],
-                rhs=codes["sq", a][:, cols].bitcast(FP8X4),
-                rhs_scale=planes["sq", a][:, cols],
-                start=False,
+                out=dst,
+                lhsT=weights,
+                lhsT_scale=weight_scales,
+                rhs=codes[name, a][:, cols].bitcast(FP8X4),
+                rhs_scale=planes[name, a][:, cols],
+                start=start,
                 stop=stop,
             )
 
-        def drain(m, cols=slice(0, T)):
-            res = stage.tile([P, T], F32, name="res")
-            if (m + (cols.stop < T)) % 2 == 0:
-                nc.scalar.copy(out=res[:, cols], in_=acc[m][:, cols])
-            else:
-                nc.vector.tensor_copy(out=res[:, cols], in_=acc[m][:, cols])
-            nc.sync.dma_start(out=out[m * P : (m + 1) * P, cols], in_=res[:, cols])
+        acc = {}
 
-        whole = slice(0, T)
-        for m in range(BANKS):
-            acc[m] = psum.tile([P, T], F32, name="acc")
-            linear_pass(0, m, slice(0, HALF), True)
-        for m in range(BANKS):
-            linear_pass(0, m, slice(HALF, T), False)
-        for m in range(BANKS):
-            square_pass(0, m, False)
-        for lo in (0, BANKS // 2):
-            for m in range(lo, lo + BANKS // 2):
-                linear_pass(1, m, whole, False)
-            for m in range(lo, lo + BANKS // 2):
-                square_pass(1, m, True)
-                drain(m)
-        for m in range(BANKS, TILES - 1):
-            acc[m] = psum.tile([P, T], F32, name="acc")
-            linear_pass(0, m, whole, True)
-            square_pass(0, m, False)
-            linear_pass(1, m, whole, False)
-            square_pass(1, m, True)
-            drain(m)
-        m = TILES - 1
-        for h in range(2):
-            acc[m] = psum.tile([P, T], F32, name="acc")
-            cols = slice(h * HALF, (h + 1) * HALF)
+        def pair_pass(name, a, i, h, start=False, stop=False):
+            if start:
+                acc[i, h] = psum.tile([P, T], F32, name="acc")
+            for u in range(2):
+                dst = acc[i, h][:, u * HALF : (u + 1) * HALF]
+                cols = slice(h * HALF, (h + 1) * HALF)
+                multiply(name, a, 2 * i + u, cols, dst, start and u == 0, stop and u == 1)
+
+        def copy_out(engine, dst, src):
+            if engine == "scalar":
+                nc.scalar.copy(out=dst, in_=src)
+            else:
+                nc.vector.tensor_copy(out=dst, in_=src)
+
+        def drain_pair(i, h, engine):
+            res = stage.tile([P, T], F32, name="res")
+            copy_out(engine, res[:], acc[i, h][:])
+            rows = out[2 * i * P : (2 * i + 2) * P, h * HALF : (h + 1) * HALF]
+            nc.sync.dma_start(
+                out=rows.rearrange("(u p) c -> p u c", u=2),
+                in_=res[:].rearrange("p (u c) -> p u c", u=2),
+            )
+
+        def whole_pair(i, h):
+            pair_pass("lin", 0, i, h, start=True)
+            pair_pass("sq", 0, i, h)
+            pair_pass("lin", 1, i, h)
+            pair_pass("sq", 1, i, h, stop=True)
+
+        def single(m, cols, engine):
+            bank = psum.tile([P, T], F32, name="acc")
+            width = cols.stop - cols.start
             for a in range(PASSES):
-                linear_pass(a, m, cols, a == 0)
-                square_pass(a, m, False, slice(cols.start, cols.start + P))
-                square_pass(a, m, a == PASSES - 1, slice(cols.start + P, cols.stop))
-            drain(m, cols)
+                multiply("lin", a, m, cols, bank[:, :width], start=a == 0)
+                multiply("sq", a, m, cols, bank[:, :width], stop=a == PASSES - 1)
+            res = stage.tile([P, T], F32, name="res")
+            copy_out(engine, res[:, :width], bank[:, :width])
+            nc.sync.dma_start(out=out[m * P : (m + 1) * P, cols], in_=res[:, :width])
+
+        load_x(0, 0)
+        load_scales(s8, w8_scales, SHIFT)
+        load_w8([0], 0, FIRST // 2)
+        load_x(0, 1)
+        load_w8([0], FIRST // 2, FIRST)
+        load_scales(s4, w4_scales, 0)
+        load_w4([0], 0, FIRST)
+        load_x(1, 0)
+        load_w8([1], 0, FIRST)
+        load_w4([1], 0, FIRST)
+        load_w8([0, 1], FIRST, TILES)
+        load_w4([0, 1], FIRST, TILES)
+        load_x(1, 1)
+
+        for a, h in ((0, 0), (0, 1), (1, 0)):
+            group("sq", a, h)
+            linear_operand(a, h)
+            quantize("sq", a, h)
+
+        pairs = range(FIRST // 2)
+        for h in range(2):
+            for i in pairs:
+                pair_pass("lin", 0, i, h, start=True)
+        for h in range(2):
+            for i in pairs:
+                pair_pass("sq", 0, i, h)
+
+        def second_pass(h, engines):
+            for i in pairs[:2]:
+                pair_pass("lin", 1, i, h)
+            for i in pairs:
+                if i >= 2:
+                    pair_pass("lin", 1, i, h)
+                pair_pass("sq", 1, i, h, stop=True)
+                drain_pair(i, h, engines[i % 2])
+
+        second_pass(0, ("scalar", "vector"))
+        group("sq", 1, 1)
+        linear_operand(1, 1)
+        whole_pair(4, 0)
+        drain_pair(4, 0, "vector")
+        quantize("sq", 1, 1)
+        whole_pair(5, 0)
+        drain_pair(5, 0, "scalar")
+        second_pass(1, ("vector", "scalar"))
+        whole_pair(4, 1)
+        drain_pair(4, 1, "vector")
+        single(TILES - 2, slice(HALF, T), "scalar")
+        single(TILES - 1, slice(HALF, T), "vector")

@@ -22,7 +22,7 @@ TILES = M // P
 BANKS = 8
 HALF = T // 2
 RUN = 4
-SHIFT = 4
+QUARTER = M // 4
 FIRST = 8
 
 
@@ -34,7 +34,7 @@ def tile_mix_feat_fm_quad_none_kernel(tc, x, w4_words, w4_scales, w8_words, w8_s
         psum = ctx.enter_context(tc.psum_pool(name="psum", bufs=BANKS))
         ctx.enter_context(tc.manual_schedule())
 
-        s8 = keep.tile([P, PASSES * M], U8, name="s8", align_bytes=64)
+        s8 = keep.tile([P, PASSES * QUARTER], U8, name="s8", align_bytes=64)
         s4 = keep.tile([P, PASSES * M], U8, name="s4", align_bytes=64)
         nc.vector.memset(s8[:].bitcast(I32), 0)
         nc.vector.memset(s4[:].bitcast(I32), 0)
@@ -47,10 +47,16 @@ def tile_mix_feat_fm_quad_none_kernel(tc, x, w4_words, w4_scales, w8_words, w8_s
             nc.sync.dma_start(out=t[:], in_=rows.rearrange("(p j) w -> p j w", j=PACK))
             raw[a, h] = t
 
-        def load_scales(plane, scales, shift):
+        def load_w4_scales():
             for r in range(4):
-                dst = plane[shift + r : P : 32, :].bitcast(I32).rearrange("q (a n) -> q a n", a=PASSES)
-                src = scales[:, r:16:4, :].rearrange("a q n -> q a n").bitcast(I32)
+                dst = s4[r:P:32, :].bitcast(I32).rearrange("q (a n) -> q a n", a=PASSES)
+                src = w4_scales[:, r:16:4, :].rearrange("a q n -> q a n").bitcast(I32)
+                nc.sync.dma_start(out=dst, in_=src)
+
+        def load_w8_scales(a):
+            for q in range(4):
+                dst = s8[32 * q : 32 * q + 16, a * QUARTER : (a + 1) * QUARTER].bitcast(I32)
+                src = w8_scales[a, 4 * q : 4 * q + 4, :].rearrange("r (c n) -> c r n", c=4).bitcast(I32)
                 nc.sync.dma_start(out=dst, in_=src)
 
         w8 = {}
@@ -116,11 +122,13 @@ def tile_mix_feat_fm_quad_none_kernel(tc, x, w4_words, w4_scales, w8_words, w8_s
                 quantize("lin", a, h, lo, lo + P)
 
         def multiply(name, a, m, cols, dst, start=False, stop=False):
-            sc = slice(a * M + m * P, a * M + (m + 1) * P)
             if name == "sq":
-                weights, weight_scales = w4[a, m].bitcast(FP4X4), s4[:, sc]
+                first = a * M + m * P
+                weights, weight_scales = w4[a, m].bitcast(FP4X4), s4[:, first : first + P]
             else:
-                weights, weight_scales = w8[a, m].bitcast(FP8X4), s8[SHIFT:, sc]
+                c, first = divmod(m * P, QUARTER)
+                first = first + a * QUARTER
+                weights, weight_scales = w8[a, m].bitcast(FP8X4), s8[4 * c :, first : first + P]
             nc.tensor.matmul_mx(
                 out=dst,
                 lhsT=weights,
@@ -173,13 +181,14 @@ def tile_mix_feat_fm_quad_none_kernel(tc, x, w4_words, w4_scales, w8_words, w8_s
             nc.sync.dma_start(out=out[m * P : (m + 1) * P, cols], in_=res[:, :width])
 
         load_x(0, 0)
-        load_scales(s8, w8_scales, SHIFT)
+        load_w8_scales(0)
         load_w8([0], 0, FIRST // 2)
         load_x(0, 1)
         load_w8([0], FIRST // 2, FIRST)
-        load_scales(s4, w4_scales, 0)
+        load_w4_scales()
         load_w4([0], 0, FIRST)
         load_x(1, 0)
+        load_w8_scales(1)
         load_w8([1], 0, FIRST)
         load_w4([1], 0, FIRST)
         load_w8([0, 1], FIRST, TILES)

@@ -24,13 +24,14 @@ HALF = T // 2
 RUN = 4
 QUARTER = M // 4
 FIRST = 8
+WARM = 6
 
 
 def tile_mix_feat_fm_quad_none_kernel(tc, x, w4_words, w4_scales, w8_words, w8_scales, out):
     nc = tc.nc
     with ExitStack() as ctx:
         keep = ctx.enter_context(tc.tile_pool(name="keep", bufs=1))
-        stage = ctx.enter_context(tc.tile_pool(name="stage", bufs=TILES + 2))
+        stage = ctx.enter_context(tc.tile_pool(name="stage", bufs=TILES + 4))
         psum = ctx.enter_context(tc.psum_pool(name="psum", bufs=BANKS))
         ctx.enter_context(tc.manual_schedule())
 
@@ -53,11 +54,11 @@ def tile_mix_feat_fm_quad_none_kernel(tc, x, w4_words, w4_scales, w8_words, w8_s
                 src = w4_scales[:, r:16:4, :].rearrange("a q n -> q a n").bitcast(I32)
                 nc.sync.dma_start(out=dst, in_=src)
 
-        def load_w8_scales(a):
+        def load_w8_scales(a, queue):
             for q in range(4):
                 dst = s8[32 * q : 32 * q + 16, a * QUARTER : (a + 1) * QUARTER].bitcast(I32)
                 src = w8_scales[a, 4 * q : 4 * q + 4, :].rearrange("r (c n) -> c r n", c=4).bitcast(I32)
-                nc.sync.dma_start(out=dst, in_=src)
+                queue.dma_start(out=dst, in_=src)
 
         w8 = {}
         w4 = {}
@@ -74,6 +75,7 @@ def tile_mix_feat_fm_quad_none_kernel(tc, x, w4_words, w4_scales, w8_words, w8_s
                 for m in range(lo, hi):
                     c = i * n + (m - lo) * P
                     w8[a, m] = t[:, c : c + P]
+            return t
 
         def load_w4(passes, lo, hi):
             n = (hi - lo) * 2 * P
@@ -170,35 +172,58 @@ def tile_mix_feat_fm_quad_none_kernel(tc, x, w4_words, w4_scales, w8_words, w8_s
             pair_pass("lin", 1, i, h)
             pair_pass("sq", 1, i, h, stop=True)
 
-        def single(m, cols, engine):
+        alone = {}
+
+        def open_single(m, cols):
             bank = psum.tile([P, T], F32, name="acc")
-            width = cols.stop - cols.start
-            for a in range(PASSES):
-                multiply("lin", a, m, cols, bank[:, :width], start=a == 0)
-                multiply("sq", a, m, cols, bank[:, :width], stop=a == PASSES - 1)
+            alone[m, cols.start] = bank[:, : cols.stop - cols.start]
+            multiply("lin", 0, m, cols, alone[m, cols.start], start=True)
+            multiply("sq", 0, m, cols, alone[m, cols.start])
+
+        def close_single(m, cols, engine):
+            multiply("lin", 1, m, cols, alone[m, cols.start])
+            multiply("sq", 1, m, cols, alone[m, cols.start], stop=True)
             res = stage.tile([P, T], F32, name="res")
-            copy_out(engine, res[:, :width], bank[:, :width])
+            width = cols.stop - cols.start
+            copy_out(engine, res[:, :width], alone[m, cols.start])
             nc.sync.dma_start(out=out[m * P : (m + 1) * P, cols], in_=res[:, :width])
 
+        first_w8 = load_w8([0], 0, 2)
+        load_w8_scales(0, nc.scalar)
         load_x(0, 0)
-        load_w8_scales(0)
-        load_w8([0], 0, FIRST // 2)
         load_x(0, 1)
-        load_w8([0], FIRST // 2, FIRST)
+        load_w8([0], 2, 5)
+        load_w8([0], 5, FIRST)
         load_w4_scales()
         load_w4([0], 0, FIRST)
         load_x(1, 0)
-        load_w8_scales(1)
+        load_w8_scales(1, nc.sync)
         load_w8([1], 0, FIRST)
         load_w4([1], 0, FIRST)
         load_w8([0, 1], FIRST, TILES)
-        load_w4([0, 1], FIRST, TILES)
         load_x(1, 1)
+        load_w4([0, 1], FIRST, TILES)
 
-        for a, h in ((0, 0), (0, 1), (1, 0)):
-            group("sq", a, h)
-            linear_operand(a, h)
-            quantize("sq", a, h)
+        unread = psum.tile([P, T], F32, name="acc")
+        for u in range(WARM):
+            nc.tensor.matmul_mx(
+                out=unread[:, :HALF],
+                lhsT=first_w8[:, :P].bitcast(FP8X4),
+                lhsT_scale=s8[:, :P],
+                rhs=first_w8[:, :HALF].bitcast(FP8X4),
+                rhs_scale=s8[:, :HALF],
+                start=True,
+                stop=True,
+            )
+
+        for h in range(2):
+            group("sq", 0, h)
+            linear_operand(0, h)
+        for h in range(2):
+            quantize("sq", 0, h)
+        group("sq", 1, 0)
+        linear_operand(1, 0)
+        quantize("sq", 1, 0)
 
         pairs = range(FIRST // 2)
         for h in range(2):
@@ -208,25 +233,32 @@ def tile_mix_feat_fm_quad_none_kernel(tc, x, w4_words, w4_scales, w8_words, w8_s
             for i in pairs:
                 pair_pass("sq", 0, i, h)
 
-        def second_pass(h, engines):
-            for i in pairs[:2]:
+        def second_pass(h, lead, engines):
+            for i in pairs[:lead]:
                 pair_pass("lin", 1, i, h)
             for i in pairs:
-                if i >= 2:
+                if i >= lead:
                     pair_pass("lin", 1, i, h)
                 pair_pass("sq", 1, i, h, stop=True)
                 drain_pair(i, h, engines[i % 2])
 
-        second_pass(0, ("scalar", "vector"))
+        second = slice(HALF, T)
+        second_pass(0, 3, ("scalar", "vector"))
         group("sq", 1, 1)
         linear_operand(1, 1)
-        whole_pair(4, 0)
-        drain_pair(4, 0, "vector")
         quantize("sq", 1, 1)
-        whole_pair(5, 0)
-        drain_pair(5, 0, "scalar")
-        second_pass(1, ("vector", "scalar"))
-        whole_pair(4, 1)
-        drain_pair(4, 1, "vector")
-        single(TILES - 2, slice(HALF, T), "scalar")
-        single(TILES - 1, slice(HALF, T), "vector")
+        late = range(FIRST // 2, TILES // 2)
+        for i in late:
+            pair_pass("lin", 0, i, 0, start=True)
+            pair_pass("lin", 1, i, 0)
+        for i in late:
+            pair_pass("sq", 0, i, 0)
+            pair_pass("sq", 1, i, 0, stop=True)
+            drain_pair(i, 0, ("scalar", "vector")[i % 2])
+        second_pass(1, 1, ("scalar", "vector"))
+        for m in range(FIRST, TILES - 1):
+            open_single(m, second)
+            close_single(m, second, ("scalar", "vector")[m % 2])
+        for cols, engine in ((slice(HALF, HALF + P), "vector"), (slice(HALF + P, T), "scalar")):
+            open_single(TILES - 1, cols)
+            close_single(TILES - 1, cols, engine)

@@ -48,17 +48,18 @@ def tile_mix_feat_fm_quad_none_kernel(tc, x, w4_words, w4_scales, w8_words, w8_s
             nc.sync.dma_start(out=t[:], in_=rows.rearrange("(p j) w -> p j w", j=PACK))
             raw[a, h] = t
 
-        def load_w4_scales():
+        def load_w4_scales(passes, lo, hi):
+            some = slice(passes[0], passes[-1] + 1)
             for r in range(4):
-                dst = s4[r:P:32, :].bitcast(I32).rearrange("q (a n) -> q a n", a=PASSES)
-                src = w4_scales[:, r:16:4, :].rearrange("a q n -> q a n").bitcast(I32)
-                nc.sync.dma_start(out=dst, in_=src)
+                dst = s4[r:P:32, :].rearrange("q (a n) -> q a n", a=PASSES)[:, some, lo * P : hi * P]
+                src = w4_scales[some, r:16:4, lo * P : hi * P].rearrange("a q n -> q a n")
+                nc.sync.dma_start(out=dst.bitcast(I32), in_=src.bitcast(I32))
 
-        def load_w8_scales(a, queue):
+        def load_w8_scales(a, queues):
             for q in range(4):
                 dst = s8[32 * q : 32 * q + 16, a * QUARTER : (a + 1) * QUARTER].bitcast(I32)
                 src = w8_scales[a, 4 * q : 4 * q + 4, :].rearrange("r (c n) -> c r n", c=4).bitcast(I32)
-                queue.dma_start(out=dst, in_=src)
+                queues[q % len(queues)].dma_start(out=dst, in_=src)
 
         w8 = {}
         w4 = {}
@@ -189,32 +190,33 @@ def tile_mix_feat_fm_quad_none_kernel(tc, x, w4_words, w4_scales, w8_words, w8_s
             nc.sync.dma_start(out=out[m * P : (m + 1) * P, cols], in_=res[:, :width])
 
         first_w8 = load_w8([0], 0, 2)
-        load_w8_scales(0, nc.scalar)
-        load_x(0, 0)
-        load_x(0, 1)
-        load_w8([0], 2, 5)
-        load_w8([0], 5, FIRST)
-        load_w4_scales()
-        load_w4([0], 0, FIRST)
-        load_x(1, 0)
-        load_w8_scales(1, nc.sync)
-        load_w8([1], 0, FIRST)
-        load_w4([1], 0, FIRST)
-        load_w8([0, 1], FIRST, TILES)
-        load_x(1, 1)
-        load_w4([0, 1], FIRST, TILES)
 
         unread = psum.tile([P, T], F32, name="acc")
         for u in range(WARM):
             nc.tensor.matmul_mx(
                 out=unread[:, :HALF],
                 lhsT=first_w8[:, :P].bitcast(FP8X4),
-                lhsT_scale=s8[:, :P],
+                lhsT_scale=s8[:, QUARTER : QUARTER + P],
                 rhs=first_w8[:, :HALF].bitcast(FP8X4),
-                rhs_scale=s8[:, :HALF],
+                rhs_scale=s8[:, QUARTER : QUARTER + HALF],
                 start=True,
                 stop=True,
             )
+
+        load_x(0, 0)
+        load_w8_scales(0, [nc.sync])
+        load_x(0, 1)
+        load_w8([0], 2, 5)
+        load_w8([0], 5, 8)
+        load_w4_scales([0, 1], 0, 12)
+        load_w4([0], 0, 8)
+        load_x(1, 0)
+        load_w8_scales(1, [nc.sync])
+        load_w8([1], 0, 8)
+        load_w4([1], 0, 8)
+        load_w8([0, 1], 8, 12)
+        load_x(1, 1)
+        load_w4([0, 1], 8, 12)
 
         for h in range(2):
             group("sq", 0, h)
@@ -255,7 +257,7 @@ def tile_mix_feat_fm_quad_none_kernel(tc, x, w4_words, w4_scales, w8_words, w8_s
             pair_pass("sq", 0, i, 0)
             pair_pass("sq", 1, i, 0, stop=True)
             drain_pair(i, 0, ("scalar", "vector")[i % 2])
-        second_pass(1, 1, ("scalar", "vector"))
+        second_pass(1, 2, ("scalar", "vector"))
         for m in range(FIRST, TILES - 1):
             open_single(m, second)
             close_single(m, second, ("scalar", "vector")[m % 2])

@@ -32,6 +32,7 @@ def tile_mix_feat_fm_quad_none_kernel(tc, x, w4_words, w4_scales, w8_words, w8_s
     with ExitStack() as ctx:
         keep = ctx.enter_context(tc.tile_pool(name="keep", bufs=1))
         stage = ctx.enter_context(tc.tile_pool(name="stage", bufs=TILES + 4))
+        wide = ctx.enter_context(tc.tile_pool(name="wide", bufs=6))
         psum = ctx.enter_context(tc.psum_pool(name="psum", bufs=BANKS))
         ctx.enter_context(tc.manual_schedule())
 
@@ -48,12 +49,12 @@ def tile_mix_feat_fm_quad_none_kernel(tc, x, w4_words, w4_scales, w8_words, w8_s
             nc.sync.dma_start(out=t[:], in_=rows.rearrange("(p j) w -> p j w", j=PACK))
             raw[a, h] = t
 
-        def load_w4_scales(passes, lo, hi):
+        def load_w4_scales(passes, lo, hi, queue=nc.sync):
             some = slice(passes[0], passes[-1] + 1)
             for r in range(4):
                 dst = s4[r:P:32, :].rearrange("q (a n) -> q a n", a=PASSES)[:, some, lo * P : hi * P]
                 src = w4_scales[some, r:16:4, lo * P : hi * P].rearrange("a q n -> q a n")
-                nc.sync.dma_start(out=dst.bitcast(I32), in_=src.bitcast(I32))
+                queue.dma_start(out=dst.bitcast(I32), in_=src.bitcast(I32))
 
         def load_w8_scales(a, queues):
             for q in range(4):
@@ -167,6 +168,16 @@ def tile_mix_feat_fm_quad_none_kernel(tc, x, w4_words, w4_scales, w8_words, w8_s
                 in_=res[:].rearrange("p (u c) -> p u c", u=2),
             )
 
+        def drain_two(i, h, engines):
+            res = wide.tile([P, 2 * T], F32, name="wide")
+            for u in range(2):
+                copy_out(engines[u], res[:, u * T : (u + 1) * T], acc[i + u, h][:])
+            rows = out[2 * i * P : (2 * i + 4) * P, h * HALF : (h + 1) * HALF]
+            nc.sync.dma_start(
+                out=rows.rearrange("(u p) c -> p u c", u=4),
+                in_=res[:].rearrange("p (u c) -> p u c", u=4),
+            )
+
         def whole_pair(i, h):
             pair_pass("lin", 0, i, h, start=True)
             pair_pass("sq", 0, i, h)
@@ -189,7 +200,7 @@ def tile_mix_feat_fm_quad_none_kernel(tc, x, w4_words, w4_scales, w8_words, w8_s
             copy_out(engine, res[:, :width], alone[m, cols.start])
             nc.sync.dma_start(out=out[m * P : (m + 1) * P, cols], in_=res[:, :width])
 
-        first_w8 = load_w8([0], 0, 2)
+        first_w8 = load_w8([0], 0, 4)
 
         unread = psum.tile([P, T], F32, name="acc")
         for u in range(WARM):
@@ -206,8 +217,7 @@ def tile_mix_feat_fm_quad_none_kernel(tc, x, w4_words, w4_scales, w8_words, w8_s
         load_x(0, 0)
         load_w8_scales(0, [nc.sync])
         load_x(0, 1)
-        load_w8([0], 2, 5)
-        load_w8([0], 5, 8)
+        load_w8([0], 4, 8)
         load_w4_scales([0, 1], 0, 12)
         load_w4([0], 0, 8)
         load_x(1, 0)
@@ -228,6 +238,8 @@ def tile_mix_feat_fm_quad_none_kernel(tc, x, w4_words, w4_scales, w8_words, w8_s
         quantize("sq", 1, 0)
 
         pairs = range(FIRST // 2)
+        late = range(FIRST // 2, TILES // 2)
+        second = slice(HALF, T)
         for h in range(2):
             for i in pairs:
                 pair_pass("lin", 0, i, h, start=True)
@@ -244,12 +256,10 @@ def tile_mix_feat_fm_quad_none_kernel(tc, x, w4_words, w4_scales, w8_words, w8_s
                 pair_pass("sq", 1, i, h, stop=True)
                 drain_pair(i, h, engines[i % 2])
 
-        second = slice(HALF, T)
         second_pass(0, 3, ("scalar", "vector"))
         group("sq", 1, 1)
         linear_operand(1, 1)
         quantize("sq", 1, 1)
-        late = range(FIRST // 2, TILES // 2)
         for i in late:
             pair_pass("lin", 0, i, 0, start=True)
             pair_pass("lin", 1, i, 0)
@@ -257,7 +267,7 @@ def tile_mix_feat_fm_quad_none_kernel(tc, x, w4_words, w4_scales, w8_words, w8_s
             pair_pass("sq", 0, i, 0)
             pair_pass("sq", 1, i, 0, stop=True)
             drain_pair(i, 0, ("scalar", "vector")[i % 2])
-        second_pass(1, 2, ("scalar", "vector"))
+        second_pass(1, 1, ("scalar", "vector"))
         for m in range(FIRST, TILES - 1):
             open_single(m, second)
             close_single(m, second, ("scalar", "vector")[m % 2])

@@ -24,7 +24,6 @@ HALF = T // 2
 RUN = 4
 QUARTER = M // 4
 FIRST = 8
-WARM = 6
 
 
 def tile_mix_feat_fm_quad_none_kernel(tc, x, w4_words, w4_scales, w8_words, w8_scales, out):
@@ -36,15 +35,15 @@ def tile_mix_feat_fm_quad_none_kernel(tc, x, w4_words, w4_scales, w8_words, w8_s
         psum = ctx.enter_context(tc.psum_pool(name="psum", bufs=BANKS))
         ctx.enter_context(tc.manual_schedule())
 
-        s8 = keep.tile([P, PASSES * QUARTER], U8, name="s8", align_bytes=64)
-        s4 = keep.tile([P, PASSES * M], U8, name="s4", align_bytes=64)
+        s8 = keep.tile([P, PASSES * QUARTER], U8, name="s8", align_bytes=256)
+        s4 = keep.tile([P, PASSES * M], U8, name="s4", align_bytes=256)
         nc.vector.memset(s8[:].bitcast(I32), 0)
         nc.vector.memset(s4[:].bitcast(I32), 0)
 
         raw = {}
 
         def load_x(a, h):
-            t = keep.tile([P, PACK, HALF], F32, name="raw_%d_%d" % (a, h), align_bytes=64)
+            t = keep.tile([P, PACK, HALF], F32, name="raw_%d_%d" % (a, h), align_bytes=256)
             rows = x[a * K_PASS : (a + 1) * K_PASS, h * HALF : (h + 1) * HALF]
             nc.sync.dma_start(out=t[:], in_=rows.rearrange("(p j) w -> p j w", j=PACK))
             raw[a, h] = t
@@ -67,7 +66,7 @@ def tile_mix_feat_fm_quad_none_kernel(tc, x, w4_words, w4_scales, w8_words, w8_s
 
         def load_w8(passes, lo, hi):
             n = (hi - lo) * P
-            t = keep.tile([P, len(passes) * n], U32, name="w8_%d_%d" % (passes[0], lo), align_bytes=64)
+            t = keep.tile([P, len(passes) * n], U32, name="w8_%d_%d" % (passes[0], lo), align_bytes=256)
             src = w8_words[passes[0] : passes[-1] + 1].rearrange("a p n i -> p a (n i)")
             nc.sync.dma_start(
                 out=t[:].bitcast(I32).rearrange("p (a n) -> p a n", a=len(passes)),
@@ -81,7 +80,7 @@ def tile_mix_feat_fm_quad_none_kernel(tc, x, w4_words, w4_scales, w8_words, w8_s
 
         def load_w4(passes, lo, hi):
             n = (hi - lo) * 2 * P
-            t = keep.tile([P, len(passes) * n], U8, name="w4_%d_%d" % (passes[0], lo), align_bytes=64)
+            t = keep.tile([P, len(passes) * n], U8, name="w4_%d_%d" % (passes[0], lo), align_bytes=256)
             src = w4_words[passes[0] : passes[-1] + 1].rearrange("a p b -> p a b")
             nc.sync.dma_start(
                 out=t[:].bitcast(I32).rearrange("p (a n) -> p a n", a=len(passes)),
@@ -96,13 +95,13 @@ def tile_mix_feat_fm_quad_none_kernel(tc, x, w4_words, w4_scales, w8_words, w8_s
         planes = {}
         for name in ("sq", "lin"):
             for a in range(PASSES):
-                codes[name, a] = keep.tile([P, T], U32, name="codes_%s_%d" % (name, a), align_bytes=64)
-                planes[name, a] = keep.tile([P, T], U8, name="plane_%s_%d" % (name, a), align_bytes=64)
+                codes[name, a] = keep.tile([P, T], U32, name="codes_%s_%d" % (name, a), align_bytes=256)
+                planes[name, a] = keep.tile([P, T], U8, name="plane_%s_%d" % (name, a), align_bytes=256)
 
         grouped = {}
 
         def group(name, a, h, lo=0, hi=HALF):
-            g = keep.tile([P, hi - lo, PACK], BF16, name="g_%s_%d_%d_%d" % (name, a, h, lo), align_bytes=64)
+            g = keep.tile([P, hi - lo, PACK], BF16, name="g_%s_%d_%d_%d" % (name, a, h, lo), align_bytes=256)
             dst = g[:].rearrange("p (c i) j -> p c j i", i=RUN)
             src = raw[a, h][:, :, lo:hi].rearrange("p j (c i) -> p c j i", i=RUN)
             if name == "sq":
@@ -160,7 +159,7 @@ def tile_mix_feat_fm_quad_none_kernel(tc, x, w4_words, w4_scales, w8_words, w8_s
                 nc.vector.tensor_copy(out=dst, in_=src)
 
         def drain_pair(i, h, engine):
-            res = stage.tile([P, T], F32, name="res")
+            res = stage.tile([P, T], F32, name="res", align_bytes=256)
             copy_out(engine, res[:], acc[i, h][:])
             rows = out[2 * i * P : (2 * i + 2) * P, h * HALF : (h + 1) * HALF]
             nc.sync.dma_start(
@@ -169,7 +168,7 @@ def tile_mix_feat_fm_quad_none_kernel(tc, x, w4_words, w4_scales, w8_words, w8_s
             )
 
         def drain_two(i, h, engines):
-            res = wide.tile([P, 2 * T], F32, name="wide")
+            res = wide.tile([P, 2 * T], F32, name="wide", align_bytes=256)
             for u in range(2):
                 copy_out(engines[u], res[:, u * T : (u + 1) * T], acc[i + u, h][:])
             rows = out[2 * i * P : (2 * i + 4) * P, h * HALF : (h + 1) * HALF]
@@ -195,27 +194,14 @@ def tile_mix_feat_fm_quad_none_kernel(tc, x, w4_words, w4_scales, w8_words, w8_s
         def close_single(m, cols, engine):
             multiply("lin", 1, m, cols, alone[m, cols.start])
             multiply("sq", 1, m, cols, alone[m, cols.start], stop=True)
-            res = stage.tile([P, T], F32, name="res")
+            res = stage.tile([P, T], F32, name="res", align_bytes=256)
             width = cols.stop - cols.start
             copy_out(engine, res[:, :width], alone[m, cols.start])
             nc.sync.dma_start(out=out[m * P : (m + 1) * P, cols], in_=res[:, :width])
 
-        first_w8 = load_w8([0], 0, 4)
-
-        unread = psum.tile([P, T], F32, name="acc")
-        for u in range(WARM):
-            nc.tensor.matmul_mx(
-                out=unread[:, :HALF],
-                lhsT=first_w8[:, :P].bitcast(FP8X4),
-                lhsT_scale=s8[:, QUARTER : QUARTER + P],
-                rhs=first_w8[:, :HALF].bitcast(FP8X4),
-                rhs_scale=s8[:, QUARTER : QUARTER + HALF],
-                start=True,
-                stop=True,
-            )
-
         load_x(0, 0)
         load_w8_scales(0, [nc.sync])
+        load_w8([0], 0, 4)
         load_x(0, 1)
         load_w8([0], 4, 8)
         load_w4_scales([0, 1], 0, 12)

@@ -22,86 +22,97 @@ TILES = M // P
 BANKS = 8
 HALF = T // 2
 RUN = 4
-QUARTER = M // 4
-FIRST = 8
+SHIFTS = 4
+SHIFT_COLS = M // SHIFTS
+EARLY = 8
+ALIGN = 256
+LEAD = (3, 1)
 
 
 def tile_mix_feat_fm_quad_none_kernel(tc, x, w4_words, w4_scales, w8_words, w8_scales, out):
     nc = tc.nc
+    early_pairs = range(EARLY // 2)
+    late_pairs = range(EARLY // 2, TILES // 2)
+    stores = 2 * len(early_pairs) + len(late_pairs) + (TILES - EARLY) + 1
+
     with ExitStack() as ctx:
         keep = ctx.enter_context(tc.tile_pool(name="keep", bufs=1))
-        stage = ctx.enter_context(tc.tile_pool(name="stage", bufs=TILES + 4))
-        wide = ctx.enter_context(tc.tile_pool(name="wide", bufs=6))
+        stage = ctx.enter_context(tc.tile_pool(name="stage", bufs=stores))
         psum = ctx.enter_context(tc.psum_pool(name="psum", bufs=BANKS))
         ctx.enter_context(tc.manual_schedule())
 
-        s8 = keep.tile([P, PASSES * QUARTER], U8, name="s8", align_bytes=256)
-        s4 = keep.tile([P, PASSES * M], U8, name="s4", align_bytes=256)
+        s8 = keep.tile([P, PASSES * SHIFT_COLS], U8, name="s8", align_bytes=ALIGN)
+        s4 = keep.tile([P, PASSES * M], U8, name="s4", align_bytes=ALIGN)
         nc.vector.memset(s8[:].bitcast(I32), 0)
         nc.vector.memset(s4[:].bitcast(I32), 0)
 
         raw = {}
+        w8 = {}
+        w4 = {}
 
         def load_x(a, h):
-            t = keep.tile([P, PACK, HALF], F32, name="raw_%d_%d" % (a, h), align_bytes=256)
+            t = keep.tile([P, PACK, HALF], F32, name="raw_%d_%d" % (a, h), align_bytes=ALIGN)
             rows = x[a * K_PASS : (a + 1) * K_PASS, h * HALF : (h + 1) * HALF]
             nc.sync.dma_start(out=t[:], in_=rows.rearrange("(p j) w -> p j w", j=PACK))
             raw[a, h] = t
 
-        def load_w4_scales(passes, lo, hi, queue=nc.sync):
-            some = slice(passes[0], passes[-1] + 1)
+        def load_w4_scales():
             for r in range(4):
-                dst = s4[r:P:32, :].rearrange("q (a n) -> q a n", a=PASSES)[:, some, lo * P : hi * P]
-                src = w4_scales[some, r:16:4, lo * P : hi * P].rearrange("a q n -> q a n")
-                queue.dma_start(out=dst.bitcast(I32), in_=src.bitcast(I32))
+                dst = s4[r:P:32, :].rearrange("q (a n) -> q a n", a=PASSES)
+                src = w4_scales[:, r:16:4, :].rearrange("a q n -> q a n")
+                nc.sync.dma_start(out=dst.bitcast(I32), in_=src.bitcast(I32))
 
-        def load_w8_scales(a, queues):
+        def load_w8_scales(a):
             for q in range(4):
-                dst = s8[32 * q : 32 * q + 16, a * QUARTER : (a + 1) * QUARTER].bitcast(I32)
-                src = w8_scales[a, 4 * q : 4 * q + 4, :].rearrange("r (c n) -> c r n", c=4).bitcast(I32)
-                queues[q % len(queues)].dma_start(out=dst, in_=src)
+                dst = s8[32 * q : 32 * q + 16, a * SHIFT_COLS : (a + 1) * SHIFT_COLS].bitcast(I32)
+                src = w8_scales[a, 4 * q : 4 * q + 4, :].rearrange("r (c n) -> c r n", c=SHIFTS).bitcast(I32)
+                nc.sync.dma_start(out=dst, in_=src)
 
-        w8 = {}
-        w4 = {}
+        def load_words(name, words, views, word_bytes, passes, lo, hi):
+            width = (hi - lo) * P * word_bytes
+            t = keep.tile([P, len(passes) * width], U8, name="%s_%d_%d" % (name, passes[0], lo), align_bytes=ALIGN)
+            src = words[passes[0] : passes[-1] + 1, :, lo * P * word_bytes : hi * P * word_bytes]
+            nc.sync.dma_start(
+                out=t[:].bitcast(I32).rearrange("p (a n) -> p a n", a=len(passes)),
+                in_=src.rearrange("a p b -> p a b").bitcast(I32),
+            )
+            for i, a in enumerate(passes):
+                for m in range(lo, hi):
+                    first = i * width + (m - lo) * P * word_bytes
+                    views[a, m] = t[:, first : first + P * word_bytes]
 
         def load_w8(passes, lo, hi):
-            n = (hi - lo) * P
-            t = keep.tile([P, len(passes) * n], U32, name="w8_%d_%d" % (passes[0], lo), align_bytes=256)
-            src = w8_words[passes[0] : passes[-1] + 1].rearrange("a p n i -> p a (n i)")
-            nc.sync.dma_start(
-                out=t[:].bitcast(I32).rearrange("p (a n) -> p a n", a=len(passes)),
-                in_=src[:, :, PACK * lo * P : PACK * hi * P].bitcast(I32),
-            )
-            for i, a in enumerate(passes):
-                for m in range(lo, hi):
-                    c = i * n + (m - lo) * P
-                    w8[a, m] = t[:, c : c + P]
-            return t
+            load_words("w8", w8_words.rearrange("a p n i -> a p (n i)"), w8, 4, passes, lo, hi)
 
         def load_w4(passes, lo, hi):
-            n = (hi - lo) * 2 * P
-            t = keep.tile([P, len(passes) * n], U8, name="w4_%d_%d" % (passes[0], lo), align_bytes=256)
-            src = w4_words[passes[0] : passes[-1] + 1].rearrange("a p b -> p a b")
-            nc.sync.dma_start(
-                out=t[:].bitcast(I32).rearrange("p (a n) -> p a n", a=len(passes)),
-                in_=src[:, :, 2 * lo * P : 2 * hi * P].bitcast(I32),
-            )
-            for i, a in enumerate(passes):
-                for m in range(lo, hi):
-                    c = i * n + (m - lo) * 2 * P
-                    w4[a, m] = t[:, c : c + 2 * P]
+            load_words("w4", w4_words, w4, 2, passes, lo, hi)
+
+        load_x(0, 0)
+        load_w8_scales(0)
+        load_w8([0], 0, EARLY // 2)
+        load_x(0, 1)
+        load_w8([0], EARLY // 2, EARLY)
+        load_w4_scales()
+        load_w4([0], 0, EARLY)
+        load_x(1, 0)
+        load_w8_scales(1)
+        load_w8([1], 0, EARLY)
+        load_w4([1], 0, EARLY)
+        load_w8([0, 1], EARLY, TILES)
+        load_x(1, 1)
+        load_w4([0, 1], EARLY, TILES)
 
         codes = {}
         planes = {}
         for name in ("sq", "lin"):
             for a in range(PASSES):
-                codes[name, a] = keep.tile([P, T], U32, name="codes_%s_%d" % (name, a), align_bytes=256)
-                planes[name, a] = keep.tile([P, T], U8, name="plane_%s_%d" % (name, a), align_bytes=256)
+                codes[name, a] = keep.tile([P, T], U32, name="codes_%s_%d" % (name, a), align_bytes=ALIGN)
+                planes[name, a] = keep.tile([P, T], U8, name="plane_%s_%d" % (name, a), align_bytes=ALIGN)
 
         grouped = {}
 
         def group(name, a, h, lo=0, hi=HALF):
-            g = keep.tile([P, hi - lo, PACK], BF16, name="g_%s_%d_%d_%d" % (name, a, h, lo), align_bytes=256)
+            g = keep.tile([P, hi - lo, PACK], BF16, name="g_%s_%d_%d_%d" % (name, a, h, lo), align_bytes=ALIGN)
             dst = g[:].rearrange("p (c i) j -> p c j i", i=RUN)
             src = raw[a, h][:, :, lo:hi].rearrange("p j (c i) -> p c j i", i=RUN)
             if name == "sq":
@@ -129,8 +140,8 @@ def tile_mix_feat_fm_quad_none_kernel(tc, x, w4_words, w4_scales, w8_words, w8_s
                 first = a * M + m * P
                 weights, weight_scales = w4[a, m].bitcast(FP4X4), s4[:, first : first + P]
             else:
-                c, first = divmod(m * P, QUARTER)
-                first = first + a * QUARTER
+                c, offset = divmod(m * P, SHIFT_COLS)
+                first = a * SHIFT_COLS + offset
                 weights, weight_scales = w8[a, m].bitcast(FP8X4), s8[4 * c :, first : first + P]
             nc.tensor.matmul_mx(
                 out=dst,
@@ -144,75 +155,43 @@ def tile_mix_feat_fm_quad_none_kernel(tc, x, w4_words, w4_scales, w8_words, w8_s
 
         acc = {}
 
-        def pair_pass(name, a, i, h, start=False, stop=False):
+        def pair_pass(name, a, i, h, start=False, stop=False, lo=0, hi=HALF):
             if start:
                 acc[i, h] = psum.tile([P, T], F32, name="acc")
+            cols = slice(h * HALF + lo, h * HALF + hi)
             for u in range(2):
-                dst = acc[i, h][:, u * HALF : (u + 1) * HALF]
-                cols = slice(h * HALF, (h + 1) * HALF)
+                dst = acc[i, h][:, u * HALF + lo : u * HALF + hi]
                 multiply(name, a, 2 * i + u, cols, dst, start and u == 0, stop and u == 1)
 
-        def copy_out(engine, dst, src):
-            if engine == "scalar":
+        def copy_out(turn, dst, src):
+            if turn % 2 == 0:
                 nc.scalar.copy(out=dst, in_=src)
             else:
                 nc.vector.tensor_copy(out=dst, in_=src)
 
-        def drain_pair(i, h, engine):
-            res = stage.tile([P, T], F32, name="res", align_bytes=256)
-            copy_out(engine, res[:], acc[i, h][:])
+        def store_pair(i, h, turn):
+            res = stage.tile([P, T], F32, name="res", align_bytes=ALIGN)
+            copy_out(turn, res[:], acc[i, h][:])
             rows = out[2 * i * P : (2 * i + 2) * P, h * HALF : (h + 1) * HALF]
             nc.sync.dma_start(
                 out=rows.rearrange("(u p) c -> p u c", u=2),
                 in_=res[:].rearrange("p (u c) -> p u c", u=2),
             )
 
-        def drain_two(i, h, engines):
-            res = wide.tile([P, 2 * T], F32, name="wide", align_bytes=256)
-            for u in range(2):
-                copy_out(engines[u], res[:, u * T : (u + 1) * T], acc[i + u, h][:])
-            rows = out[2 * i * P : (2 * i + 4) * P, h * HALF : (h + 1) * HALF]
-            nc.sync.dma_start(
-                out=rows.rearrange("(u p) c -> p u c", u=4),
-                in_=res[:].rearrange("p (u c) -> p u c", u=4),
-            )
-
-        def whole_pair(i, h):
-            pair_pass("lin", 0, i, h, start=True)
-            pair_pass("sq", 0, i, h)
-            pair_pass("lin", 1, i, h)
-            pair_pass("sq", 1, i, h, stop=True)
-
-        alone = {}
-
-        def open_single(m, cols):
-            bank = psum.tile([P, T], F32, name="acc")
-            alone[m, cols.start] = bank[:, : cols.stop - cols.start]
-            multiply("lin", 0, m, cols, alone[m, cols.start], start=True)
-            multiply("sq", 0, m, cols, alone[m, cols.start])
-
-        def close_single(m, cols, engine):
-            multiply("lin", 1, m, cols, alone[m, cols.start])
-            multiply("sq", 1, m, cols, alone[m, cols.start], stop=True)
-            res = stage.tile([P, T], F32, name="res", align_bytes=256)
+        def single(m, cols, turn):
             width = cols.stop - cols.start
-            copy_out(engine, res[:, :width], alone[m, cols.start])
+            bank = psum.tile([P, T], F32, name="acc")
+            for a in range(PASSES):
+                multiply("lin", a, m, cols, bank[:, :width], start=a == 0)
+                multiply("sq", a, m, cols, bank[:, :width], stop=a == PASSES - 1)
+            res = stage.tile([P, T], F32, name="res", align_bytes=ALIGN)
+            copy_out(turn, res[:, :width], bank[:, :width])
             nc.sync.dma_start(out=out[m * P : (m + 1) * P, cols], in_=res[:, :width])
 
-        load_x(0, 0)
-        load_w8_scales(0, [nc.sync])
-        load_w8([0], 0, 4)
-        load_x(0, 1)
-        load_w8([0], 4, 8)
-        load_w4_scales([0, 1], 0, 12)
-        load_w4([0], 0, 8)
-        load_x(1, 0)
-        load_w8_scales(1, [nc.sync])
-        load_w8([1], 0, 8)
-        load_w4([1], 0, 8)
-        load_w8([0, 1], 8, 12)
-        load_x(1, 1)
-        load_w4([0, 1], 8, 12)
+        def close_pair(i, h):
+            if i >= LEAD[h]:
+                pair_pass("lin", 1, i, h)
+            pair_pass("sq", 1, i, h, stop=True)
 
         for h in range(2):
             group("sq", 0, h)
@@ -223,40 +202,42 @@ def tile_mix_feat_fm_quad_none_kernel(tc, x, w4_words, w4_scales, w8_words, w8_s
         linear_operand(1, 0)
         quantize("sq", 1, 0)
 
-        pairs = range(FIRST // 2)
-        late = range(FIRST // 2, TILES // 2)
-        second = slice(HALF, T)
+        for lo in (0, P):
+            for i in early_pairs[:2]:
+                pair_pass("lin", 0, i, 0, start=lo == 0, lo=lo, hi=lo + P)
+        for i in early_pairs[2:]:
+            pair_pass("lin", 0, i, 0, start=True)
+        for i in early_pairs:
+            pair_pass("lin", 0, i, 1, start=True)
         for h in range(2):
-            for i in pairs:
-                pair_pass("lin", 0, i, h, start=True)
-        for h in range(2):
-            for i in pairs:
+            for i in early_pairs:
                 pair_pass("sq", 0, i, h)
 
-        def second_pass(h, lead, engines):
-            for i in pairs[:lead]:
-                pair_pass("lin", 1, i, h)
-            for i in pairs:
-                if i >= lead:
-                    pair_pass("lin", 1, i, h)
-                pair_pass("sq", 1, i, h, stop=True)
-                drain_pair(i, h, engines[i % 2])
-
-        second_pass(0, 3, ("scalar", "vector"))
-        group("sq", 1, 1)
+        for i in early_pairs[: LEAD[0]]:
+            pair_pass("lin", 1, i, 0)
+        for i in early_pairs:
+            close_pair(i, 0)
+            if i == early_pairs[-1]:
+                group("sq", 1, 1)
+            store_pair(i, 0, i + 1)
         linear_operand(1, 1)
         quantize("sq", 1, 1)
-        for i in late:
-            pair_pass("lin", 0, i, 0, start=True)
-            pair_pass("lin", 1, i, 0)
-        for i in late:
-            pair_pass("sq", 0, i, 0)
-            pair_pass("sq", 1, i, 0, stop=True)
-            drain_pair(i, 0, ("scalar", "vector")[i % 2])
-        second_pass(1, 1, ("scalar", "vector"))
-        for m in range(FIRST, TILES - 1):
-            open_single(m, second)
-            close_single(m, second, ("scalar", "vector")[m % 2])
-        for cols, engine in ((slice(HALF, HALF + P), "vector"), (slice(HALF + P, T), "scalar")):
-            open_single(TILES - 1, cols)
-            close_single(TILES - 1, cols, engine)
+
+        for i in late_pairs:
+            for a in range(PASSES):
+                pair_pass("lin", a, i, 0, start=a == 0)
+        for i in late_pairs:
+            for a in range(PASSES):
+                pair_pass("sq", a, i, 0, stop=a == PASSES - 1)
+            store_pair(i, 0, i)
+
+        for i in early_pairs[: LEAD[1]]:
+            pair_pass("lin", 1, i, 1)
+        for i in early_pairs:
+            close_pair(i, 1)
+            store_pair(i, 1, i)
+
+        for m in range(EARLY, TILES - 1):
+            single(m, slice(HALF, T), m)
+        for u in range(2):
+            single(TILES - 1, slice(HALF + u * P, HALF + (u + 1) * P), TILES - 1 + u)

@@ -13,6 +13,7 @@ U8 = mybir.dt.uint8
 FP8X4 = mybir.dt.float8_e4m3fn_x4
 FP4X4 = mybir.dt.float4_e2m1fn_x4
 SQUARE = mybir.ActivationFunctionType.Square
+MULT = mybir.AluOpType.mult
 
 P = 128
 PACK = 4
@@ -95,9 +96,9 @@ def tile_mix_feat_fm_quad_none_kernel(tc, x, w4_words, w4_scales, w8_words, w8_s
         load_w4_scales()
         load_w4([0], 0, EARLY)
         load_x(1, 0)
+        load_w4([1], 0, EARLY)
         load_w8_scales(1)
         load_w8([1], 0, EARLY)
-        load_w4([1], 0, EARLY)
         load_w8([0, 1], EARLY, TILES)
         load_x(1, 1)
         load_w4([0, 1], EARLY, TILES)
@@ -111,11 +112,13 @@ def tile_mix_feat_fm_quad_none_kernel(tc, x, w4_words, w4_scales, w8_words, w8_s
 
         grouped = {}
 
-        def group(name, a, h, lo=0, hi=HALF):
+        def group(name, a, h, lo=0, hi=HALF, on_vector=False):
             g = keep.tile([P, hi - lo, PACK], BF16, name="g_%s_%d_%d_%d" % (name, a, h, lo), align_bytes=ALIGN)
             dst = g[:].rearrange("p (c i) j -> p c j i", i=RUN)
             src = raw[a, h][:, :, lo:hi].rearrange("p j (c i) -> p c j i", i=RUN)
-            if name == "sq":
+            if name == "sq" and on_vector:
+                nc.vector.tensor_tensor(out=dst, in0=src, in1=src, op=MULT)
+            elif name == "sq":
                 nc.scalar.activation(out=dst, in_=src, func=SQUARE)
             else:
                 nc.vector.tensor_copy(out=dst, in_=src)
@@ -198,9 +201,14 @@ def tile_mix_feat_fm_quad_none_kernel(tc, x, w4_words, w4_scales, w8_words, w8_s
             linear_operand(0, h)
         for h in range(2):
             quantize("sq", 0, h)
-        group("sq", 1, 0)
-        linear_operand(1, 0)
-        quantize("sq", 1, 0)
+        group("sq", 1, 0, 0, P)
+        group("sq", 1, 0, P, HALF, on_vector=True)
+        group("lin", 1, 0, 0, P)
+        for lo in (P, 0):
+            quantize("sq", 1, 0, lo, lo + P)
+        group("lin", 1, 0, P, HALF)
+        for lo in (0, P):
+            quantize("lin", 1, 0, lo, lo + P)
 
         for lo in (0, P):
             for i in early_pairs[:2]:
@@ -214,9 +222,11 @@ def tile_mix_feat_fm_quad_none_kernel(tc, x, w4_words, w4_scales, w8_words, w8_s
                 pair_pass("sq", 0, i, h)
 
         for i in early_pairs[: LEAD[0]]:
-            pair_pass("lin", 1, i, 0)
+            pair_pass("sq", 1, i, 0)
         for i in early_pairs:
-            close_pair(i, 0)
+            if i >= LEAD[0]:
+                pair_pass("sq", 1, i, 0)
+            pair_pass("lin", 1, i, 0, stop=True)
             if i == early_pairs[-1]:
                 group("sq", 1, 1)
             store_pair(i, 0, i + 1)

@@ -27,18 +27,20 @@ SHIFTS = 4
 SHIFT_COLS = M // SHIFTS
 EARLY = 8
 ALIGN = 256
-LEAD = (3, 1)
+LEAD = 2
 
 
 def tile_mix_feat_fm_quad_none_kernel(tc, x, w4_words, w4_scales, w8_words, w8_scales, out):
     nc = tc.nc
-    early_pairs = range(EARLY // 2)
-    late_pairs = range(EARLY // 2, TILES // 2)
-    stores = 2 * len(early_pairs) + len(late_pairs) + (TILES - EARLY) + 1
+    whole = slice(0, T)
+    halves = (slice(0, HALF), slice(HALF, T))
+    pieces = [(m, whole) for m in range(EARLY, TILES - 2)]
+    pieces.extend([(TILES - 2, halves[0]), (TILES - 2, halves[1]), (TILES - 1, halves[0])])
+    pieces.extend([(TILES - 1, slice(HALF, HALF + P)), (TILES - 1, slice(HALF + P, T))])
 
     with ExitStack() as ctx:
         keep = ctx.enter_context(tc.tile_pool(name="keep", bufs=1))
-        stage = ctx.enter_context(tc.tile_pool(name="stage", bufs=stores))
+        stage = ctx.enter_context(tc.tile_pool(name="stage", bufs=2 + len(pieces)))
         psum = ctx.enter_context(tc.psum_pool(name="psum", bufs=BANKS))
         ctx.enter_context(tc.manual_schedule())
 
@@ -96,11 +98,11 @@ def tile_mix_feat_fm_quad_none_kernel(tc, x, w4_words, w4_scales, w8_words, w8_s
         load_w4_scales()
         load_w4([0], 0, EARLY)
         load_x(1, 0)
+        load_x(1, 1)
         load_w4([1], 0, EARLY)
         load_w8_scales(1)
         load_w8([1], 0, EARLY)
         load_w8([0, 1], EARLY, TILES)
-        load_x(1, 1)
         load_w4([0, 1], EARLY, TILES)
 
         codes = {}
@@ -112,14 +114,16 @@ def tile_mix_feat_fm_quad_none_kernel(tc, x, w4_words, w4_scales, w8_words, w8_s
 
         grouped = {}
 
-        def group(name, a, h, lo=0, hi=HALF, on_vector=False):
+        def group(name, a, h, lo=0, hi=HALF, helper=False):
             g = keep.tile([P, hi - lo, PACK], BF16, name="g_%s_%d_%d_%d" % (name, a, h, lo), align_bytes=ALIGN)
             dst = g[:].rearrange("p (c i) j -> p c j i", i=RUN)
             src = raw[a, h][:, :, lo:hi].rearrange("p j (c i) -> p c j i", i=RUN)
-            if name == "sq" and on_vector:
+            if name == "sq" and helper:
                 nc.vector.tensor_tensor(out=dst, in0=src, in1=src, op=MULT)
             elif name == "sq":
                 nc.scalar.activation(out=dst, in_=src, func=SQUARE)
+            elif helper:
+                nc.scalar.copy(out=dst, in_=src)
             else:
                 nc.vector.tensor_copy(out=dst, in_=src)
             grouped[name, a, h, lo] = g
@@ -158,96 +162,79 @@ def tile_mix_feat_fm_quad_none_kernel(tc, x, w4_words, w4_scales, w8_words, w8_s
 
         acc = {}
 
-        def pair_pass(name, a, i, h, start=False, stop=False, lo=0, hi=HALF):
+        def tile_pass(name, a, m, cols, start=False, stop=False):
             if start:
-                acc[i, h] = psum.tile([P, T], F32, name="acc")
-            cols = slice(h * HALF + lo, h * HALF + hi)
-            for u in range(2):
-                dst = acc[i, h][:, u * HALF + lo : u * HALF + hi]
-                multiply(name, a, 2 * i + u, cols, dst, start and u == 0, stop and u == 1)
+                acc[m] = psum.tile([P, T], F32, name="acc")
+            multiply(name, a, m, cols, acc[m][:, cols], start, stop)
 
-        def copy_out(turn, dst, src):
-            if turn % 2 == 0:
-                nc.scalar.copy(out=dst, in_=src)
-            else:
-                nc.vector.tensor_copy(out=dst, in_=src)
-
-        def store_pair(i, h, turn):
-            res = stage.tile([P, T], F32, name="res", align_bytes=ALIGN)
-            copy_out(turn, res[:], acc[i, h][:])
-            rows = out[2 * i * P : (2 * i + 2) * P, h * HALF : (h + 1) * HALF]
-            nc.sync.dma_start(
-                out=rows.rearrange("(u p) c -> p u c", u=2),
-                in_=res[:].rearrange("p (u c) -> p u c", u=2),
-            )
-
-        def single(m, cols, turn):
+        def store(turn, m, cols, sums):
             width = cols.stop - cols.start
-            bank = psum.tile([P, T], F32, name="acc")
-            for a in range(PASSES):
-                multiply("lin", a, m, cols, bank[:, :width], start=a == 0)
-                multiply("sq", a, m, cols, bank[:, :width], stop=a == PASSES - 1)
             res = stage.tile([P, T], F32, name="res", align_bytes=ALIGN)
-            copy_out(turn, res[:, :width], bank[:, :width])
+            if turn % 2 == 0:
+                nc.scalar.copy(out=res[:, :width], in_=sums)
+            else:
+                nc.vector.tensor_copy(out=res[:, :width], in_=sums)
             nc.sync.dma_start(out=out[m * P : (m + 1) * P, cols], in_=res[:, :width])
 
-        def close_pair(i, h):
-            if i >= LEAD[h]:
-                pair_pass("lin", 1, i, h)
-            pair_pass("sq", 1, i, h, stop=True)
+        doubles = {}
+
+        def store_two(m):
+            if m % 2 == 0:
+                doubles[m // 2] = keep.tile([P, 2, T], F32, name="res_%d" % m, align_bytes=ALIGN)
+                nc.scalar.copy(out=doubles[m // 2][:, 0, :], in_=acc[m][:])
+            else:
+                nc.vector.tensor_copy(out=doubles[m // 2][:, 1, :], in_=acc[m][:])
+                rows = out[(m - 1) * P : (m + 1) * P, :].rearrange("(u p) c -> p u c", u=2)
+                nc.sync.dma_start(out=rows, in_=doubles[m // 2][:])
 
         for h in range(2):
             group("sq", 0, h)
             linear_operand(0, h)
         for h in range(2):
             quantize("sq", 0, h)
+
         group("sq", 1, 0, 0, P)
-        group("sq", 1, 0, P, HALF, on_vector=True)
+        group("sq", 1, 0, P, HALF, helper=True)
         group("lin", 1, 0, 0, P)
+        group("lin", 1, 0, P, HALF, helper=True)
         for lo in (P, 0):
             quantize("sq", 1, 0, lo, lo + P)
-        group("lin", 1, 0, P, HALF)
+        for lo in (0, P):
+            group("sq", 1, 1, lo, lo + P)
+        group("lin", 1, 1)
+        quantize("sq", 1, 1, 0, P)
         for lo in (0, P):
             quantize("lin", 1, 0, lo, lo + P)
+        quantize("sq", 1, 1, P, HALF)
+        quantize("lin", 1, 1)
 
         for lo in (0, P):
-            for i in early_pairs[:2]:
-                pair_pass("lin", 0, i, 0, start=lo == 0, lo=lo, hi=lo + P)
-        for i in early_pairs[2:]:
-            pair_pass("lin", 0, i, 0, start=True)
-        for i in early_pairs:
-            pair_pass("lin", 0, i, 1, start=True)
-        for h in range(2):
-            for i in early_pairs:
-                pair_pass("sq", 0, i, h)
+            for m in range(EARLY // 2):
+                tile_pass("lin", 0, m, slice(lo, lo + P), start=lo == 0)
+        for m in range(EARLY // 2, EARLY):
+            tile_pass("lin", 0, m, halves[0], start=True)
+        for m in range(EARLY):
+            tile_pass("lin", 0, m, halves[1])
+        for m in range(EARLY):
+            tile_pass("sq", 0, m, whole)
 
-        for i in early_pairs[: LEAD[0]]:
-            pair_pass("sq", 1, i, 0)
-        for i in early_pairs:
-            if i >= LEAD[0]:
-                pair_pass("sq", 1, i, 0)
-            pair_pass("lin", 1, i, 0, stop=True)
-            if i == early_pairs[-1]:
-                group("sq", 1, 1)
-            store_pair(i, 0, i + 1)
-        linear_operand(1, 1)
-        quantize("sq", 1, 1)
+        for m in range(EARLY):
+            tile_pass("sq", 1, m, halves[0])
+        for m in range(LEAD):
+            tile_pass("sq", 1, m, halves[1])
+        for m in range(EARLY):
+            if m >= LEAD:
+                tile_pass("sq", 1, m, halves[1])
+            tile_pass("lin", 1, m, whole, stop=True)
+            if m < 2:
+                store(m, m, whole, acc[m][:])
+            else:
+                store_two(m)
 
-        for i in late_pairs:
+        for turn, (m, cols) in enumerate(pieces):
+            bank = psum.tile([P, T], F32, name="acc")
+            sums = bank[:, : cols.stop - cols.start]
             for a in range(PASSES):
-                pair_pass("lin", a, i, 0, start=a == 0)
-        for i in late_pairs:
-            for a in range(PASSES):
-                pair_pass("sq", a, i, 0, stop=a == PASSES - 1)
-            store_pair(i, 0, i)
-
-        for i in early_pairs[: LEAD[1]]:
-            pair_pass("lin", 1, i, 1)
-        for i in early_pairs:
-            close_pair(i, 1)
-            store_pair(i, 1, i)
-
-        for m in range(EARLY, TILES - 1):
-            single(m, slice(HALF, T), m)
-        for u in range(2):
-            single(TILES - 1, slice(HALF + u * P, HALF + (u + 1) * P), TILES - 1 + u)
+                multiply("lin", a, m, cols, sums, start=a == 0)
+                multiply("sq", a, m, cols, sums, stop=a == PASSES - 1)
+            store(turn, m, cols, sums)

@@ -26,21 +26,24 @@ RUN = 4
 SHIFTS = 4
 SHIFT_COLS = M // SHIFTS
 EARLY = 8
+PAIRED = 4
+FILL = 2
 ALIGN = 256
-LEAD = 2
 
 
 def tile_mix_feat_fm_quad_none_kernel(tc, x, w4_words, w4_scales, w8_words, w8_scales, out):
     nc = tc.nc
     whole = slice(0, T)
     halves = (slice(0, HALF), slice(HALF, T))
+    pairs = range(PAIRED // 2)
+    singles = range(PAIRED, EARLY)
     pieces = [(m, whole) for m in range(EARLY, TILES - 2)]
     pieces.extend([(TILES - 2, halves[0]), (TILES - 2, halves[1]), (TILES - 1, halves[0])])
     pieces.extend([(TILES - 1, slice(HALF, HALF + P)), (TILES - 1, slice(HALF + P, T))])
 
     with ExitStack() as ctx:
         keep = ctx.enter_context(tc.tile_pool(name="keep", bufs=1))
-        stage = ctx.enter_context(tc.tile_pool(name="stage", bufs=2 + len(pieces)))
+        stage = ctx.enter_context(tc.tile_pool(name="stage", bufs=2 * len(pairs) + len(pieces)))
         psum = ctx.enter_context(tc.psum_pool(name="psum", bufs=BANKS))
         ctx.enter_context(tc.manual_schedule())
 
@@ -101,7 +104,8 @@ def tile_mix_feat_fm_quad_none_kernel(tc, x, w4_words, w4_scales, w8_words, w8_s
         load_x(1, 1)
         load_w4([1], 0, EARLY)
         load_w8_scales(1)
-        load_w8([1], 0, EARLY)
+        load_w8([1], 0, PAIRED)
+        load_w8([1], PAIRED, EARLY)
         load_w8([0, 1], EARLY, TILES)
         load_w4([0, 1], EARLY, TILES)
 
@@ -167,14 +171,31 @@ def tile_mix_feat_fm_quad_none_kernel(tc, x, w4_words, w4_scales, w8_words, w8_s
                 acc[m] = psum.tile([P, T], F32, name="acc")
             multiply(name, a, m, cols, acc[m][:, cols], start, stop)
 
+        def pair_pass(name, a, i, h, start=False, stop=False, lo=0, hi=HALF):
+            if start:
+                acc["pair", i, h] = psum.tile([P, T], F32, name="acc")
+            cols = slice(h * HALF + lo, h * HALF + hi)
+            for u in range(2):
+                dst = acc["pair", i, h][:, u * HALF + lo : u * HALF + hi]
+                multiply(name, a, 2 * i + u, cols, dst, start and u == 0, stop and u == 1)
+
+        def copy_out(turn, dst, src):
+            if turn % 2 == 0:
+                nc.scalar.copy(out=dst, in_=src)
+            else:
+                nc.vector.tensor_copy(out=dst, in_=src)
+
         def store(turn, m, cols, sums):
             width = cols.stop - cols.start
             res = stage.tile([P, T], F32, name="res", align_bytes=ALIGN)
-            if turn % 2 == 0:
-                nc.scalar.copy(out=res[:, :width], in_=sums)
-            else:
-                nc.vector.tensor_copy(out=res[:, :width], in_=sums)
+            copy_out(turn, res[:, :width], sums)
             nc.sync.dma_start(out=out[m * P : (m + 1) * P, cols], in_=res[:, :width])
+
+        def store_pair(turn, i, h):
+            res = stage.tile([P, T], F32, name="res", align_bytes=ALIGN)
+            copy_out(turn, res[:], acc["pair", i, h][:])
+            rows = out[2 * i * P : (2 * i + 2) * P, halves[h]].rearrange("(u p) c -> p u c", u=2)
+            nc.sync.dma_start(out=rows, in_=res[:].rearrange("p (u c) -> p u c", u=2))
 
         doubles = {}
 
@@ -193,43 +214,48 @@ def tile_mix_feat_fm_quad_none_kernel(tc, x, w4_words, w4_scales, w8_words, w8_s
         for h in range(2):
             quantize("sq", 0, h)
 
-        group("sq", 1, 0, 0, P)
-        group("sq", 1, 0, P, HALF, helper=True)
-        group("lin", 1, 0, 0, P)
-        group("lin", 1, 0, P, HALF, helper=True)
-        for lo in (P, 0):
-            quantize("sq", 1, 0, lo, lo + P)
-        for lo in (0, P):
-            group("sq", 1, 1, lo, lo + P)
-        group("lin", 1, 1)
-        quantize("sq", 1, 1, 0, P)
-        for lo in (0, P):
-            quantize("lin", 1, 0, lo, lo + P)
-        quantize("sq", 1, 1, P, HALF)
-        quantize("lin", 1, 1)
+        for h in range(2):
+            group("sq", 1, h, 0, P)
+            group("sq", 1, h, P, HALF, helper=True)
+            group("lin", 1, h, 0, P)
+            group("lin", 1, h, P, HALF, helper=True)
+            for lo in (P, 0):
+                quantize("sq", 1, h, lo, lo + P)
+            for lo in (0, P):
+                quantize("lin", 1, h, lo, lo + P)
 
         for lo in (0, P):
-            for m in range(EARLY // 2):
-                tile_pass("lin", 0, m, slice(lo, lo + P), start=lo == 0)
-        for m in range(EARLY // 2, EARLY):
+            for i in pairs:
+                pair_pass("lin", 0, i, 0, start=lo == 0, lo=lo, hi=lo + P)
+        for m in singles:
             tile_pass("lin", 0, m, halves[0], start=True)
-        for m in range(EARLY):
+        for i in pairs:
+            pair_pass("lin", 0, i, 1, start=True)
+        for m in singles:
             tile_pass("lin", 0, m, halves[1])
-        for m in range(EARLY):
+        for h in range(2):
+            for i in pairs:
+                pair_pass("sq", 0, i, h)
+        for m in singles:
             tile_pass("sq", 0, m, whole)
 
-        for m in range(EARLY):
+        for i in pairs:
+            pair_pass("sq", 1, i, 0)
+        for m in singles[:FILL]:
             tile_pass("sq", 1, m, halves[0])
-        for m in range(LEAD):
+        for i in pairs:
+            pair_pass("lin", 1, i, 0, stop=True)
+            store_pair(i, i, 0)
+        for m in singles[FILL:]:
+            tile_pass("sq", 1, m, halves[0])
+        for i in pairs:
+            pair_pass("sq", 1, i, 1)
+            pair_pass("lin", 1, i, 1, stop=True)
+            store_pair(i, i, 1)
+        for m in singles:
             tile_pass("sq", 1, m, halves[1])
-        for m in range(EARLY):
-            if m >= LEAD:
-                tile_pass("sq", 1, m, halves[1])
             tile_pass("lin", 1, m, whole, stop=True)
-            if m < 2:
-                store(m, m, whole, acc[m][:])
-            else:
-                store_two(m)
+            store_two(m)
 
         for turn, (m, cols) in enumerate(pieces):
             bank = psum.tile([P, T], F32, name="acc")

@@ -26,8 +26,7 @@ RUN = 4
 SHIFTS = 4
 SHIFT_COLS = M // SHIFTS
 EARLY = 8
-PAIRED = 4
-FILL = 2
+PAIRED = 6
 ALIGN = 256
 
 
@@ -104,8 +103,8 @@ def tile_mix_feat_fm_quad_none_kernel(tc, x, w4_words, w4_scales, w8_words, w8_s
         load_x(1, 1)
         load_w4([1], 0, EARLY)
         load_w8_scales(1)
-        load_w8([1], 0, PAIRED)
-        load_w8([1], PAIRED, EARLY)
+        load_w8([1], 0, EARLY // 2)
+        load_w8([1], EARLY // 2, EARLY)
         load_w8([0, 1], EARLY, TILES)
         load_w4([0, 1], EARLY, TILES)
 
@@ -197,22 +196,15 @@ def tile_mix_feat_fm_quad_none_kernel(tc, x, w4_words, w4_scales, w8_words, w8_s
             rows = out[2 * i * P : (2 * i + 2) * P, halves[h]].rearrange("(u p) c -> p u c", u=2)
             nc.sync.dma_start(out=rows, in_=res[:].rearrange("p (u c) -> p u c", u=2))
 
-        doubles = {}
-
-        def store_two(m):
-            if m % 2 == 0:
-                doubles[m // 2] = keep.tile([P, 2, T], F32, name="res_%d" % m, align_bytes=ALIGN)
-                nc.scalar.copy(out=doubles[m // 2][:, 0, :], in_=acc[m][:])
-            else:
-                nc.vector.tensor_copy(out=doubles[m // 2][:, 1, :], in_=acc[m][:])
-                rows = out[(m - 1) * P : (m + 1) * P, :].rearrange("(u p) c -> p u c", u=2)
-                nc.sync.dma_start(out=rows, in_=doubles[m // 2][:])
-
-        for h in range(2):
-            group("sq", 0, h)
-            linear_operand(0, h)
-        for h in range(2):
-            quantize("sq", 0, h)
+        group("sq", 0, 0)
+        linear_operand(0, 0)
+        quantize("sq", 0, 0)
+        group("lin", 0, 1, 0, P)
+        group("lin", 0, 1, P, HALF, helper=True)
+        group("sq", 0, 1)
+        for lo in (0, P):
+            quantize("lin", 0, 1, lo, lo + P)
+        quantize("sq", 0, 1)
 
         for h in range(2):
             group("sq", 1, h, 0, P)
@@ -225,8 +217,10 @@ def tile_mix_feat_fm_quad_none_kernel(tc, x, w4_words, w4_scales, w8_words, w8_s
                 quantize("lin", 1, h, lo, lo + P)
 
         for lo in (0, P):
-            for i in pairs:
+            for i in pairs[:2]:
                 pair_pass("lin", 0, i, 0, start=lo == 0, lo=lo, hi=lo + P)
+        for i in pairs[2:]:
+            pair_pass("lin", 0, i, 0, start=True)
         for m in singles:
             tile_pass("lin", 0, m, halves[0], start=True)
         for i in pairs:
@@ -241,21 +235,22 @@ def tile_mix_feat_fm_quad_none_kernel(tc, x, w4_words, w4_scales, w8_words, w8_s
 
         for i in pairs:
             pair_pass("sq", 1, i, 0)
-        for m in singles[:FILL]:
-            tile_pass("sq", 1, m, halves[0])
         for i in pairs:
             pair_pass("lin", 1, i, 0, stop=True)
             store_pair(i, i, 0)
-        for m in singles[FILL:]:
+        for m in singles:
             tile_pass("sq", 1, m, halves[0])
         for i in pairs:
             pair_pass("sq", 1, i, 1)
             pair_pass("lin", 1, i, 1, stop=True)
             store_pair(i, i, 1)
+        both = keep.tile([P, len(singles), T], F32, name="both", align_bytes=ALIGN)
         for m in singles:
             tile_pass("sq", 1, m, halves[1])
             tile_pass("lin", 1, m, whole, stop=True)
-            store_two(m)
+            copy_out(m + 1, both[:, m - PAIRED, :], acc[m][:])
+        rows = out[PAIRED * P : EARLY * P, :].rearrange("(u p) c -> p u c", u=len(singles))
+        nc.sync.dma_start(out=rows, in_=both[:])
 
         for turn, (m, cols) in enumerate(pieces):
             bank = psum.tile([P, T], F32, name="acc")

@@ -27,6 +27,8 @@ SHIFTS = 4
 SHIFT_COLS = M // SHIFTS
 EARLY = 8
 PAIRED = 6
+WARM_PASSES = 4
+TWO_ONES = 0x3F803F80
 ALIGN = 256
 
 
@@ -48,8 +50,25 @@ def tile_mix_feat_fm_quad_none_kernel(tc, x, w4_words, w4_scales, w8_words, w8_s
 
         s8 = keep.tile([P, PASSES * SHIFT_COLS], U8, name="s8", align_bytes=ALIGN)
         s4 = keep.tile([P, PASSES * M], U8, name="s4", align_bytes=ALIGN)
+        ones = keep.tile([P, PACK * T], BF16, name="ones", align_bytes=ALIGN)
         nc.vector.memset(s8[:].bitcast(I32), 0)
+        nc.vector.memset(ones[:].bitcast(I32), TWO_ONES)
+
+        warm_codes = keep.tile([P, T], U32, name="warm_codes", align_bytes=ALIGN)
+        warm_plane = keep.tile([P, T], U8, name="warm_plane", align_bytes=ALIGN)
+        nc.vector.quantize_mx(out=warm_codes[:].bitcast(FP8X4), scales=warm_plane[:], in_=ones[:])
         nc.vector.memset(s4[:].bitcast(I32), 0)
+        warm_bank = psum.tile([P, T], F32, name="acc")
+        for i in range(WARM_PASSES):
+            nc.tensor.matmul_mx(
+                out=warm_bank[:],
+                lhsT=warm_codes[:, :P].bitcast(FP8X4),
+                lhsT_scale=warm_plane[:, :P],
+                rhs=warm_codes[:].bitcast(FP8X4),
+                rhs_scale=warm_plane[:],
+                start=True,
+                stop=True,
+            )
 
         raw = {}
         w8 = {}

@@ -50,13 +50,15 @@ def tile_mix_feat_fm_quad_none_kernel(tc, x, w4_words, w4_scales, w8_words, w8_s
 
         s8 = keep.tile([P, PASSES * SHIFT_COLS], U8, name="s8", align_bytes=ALIGN)
         s4 = keep.tile([P, PASSES * M], U8, name="s4", align_bytes=ALIGN)
-        ones = keep.tile([P, PACK * T], BF16, name="ones", align_bytes=ALIGN)
-        nc.vector.memset(s8[:].bitcast(I32), 0)
+        ones = keep.tile([P, PACK * T // 4], BF16, name="ones", align_bytes=ALIGN)
         nc.vector.memset(ones[:].bitcast(I32), TWO_ONES)
+        nc.vector.memset(s8[:].bitcast(I32), 0)
 
         warm_codes = keep.tile([P, T], U32, name="warm_codes", align_bytes=ALIGN)
         warm_plane = keep.tile([P, T], U8, name="warm_plane", align_bytes=ALIGN)
-        nc.vector.quantize_mx(out=warm_codes[:].bitcast(FP8X4), scales=warm_plane[:], in_=ones[:])
+        for lo in range(0, T, T // 4):
+            cols = slice(lo, lo + T // 4)
+            nc.vector.quantize_mx(out=warm_codes[:, cols].bitcast(FP8X4), scales=warm_plane[:, cols], in_=ones[:])
         nc.vector.memset(s4[:].bitcast(I32), 0)
         warm_bank = psum.tile([P, T], F32, name="acc")
         for i in range(WARM_PASSES):

@@ -256,11 +256,11 @@ def tile_mix_feat_fm_quad_none_kernel(tc, x, w4_words, w4_scales, w8_words, w8_s
 
         for i in pairs:
             pair_pass("sq", 1, i, 0)
+        for m in singles:
+            tile_pass("sq", 1, m, halves[0])
         for i in pairs:
             pair_pass("lin", 1, i, 0, stop=True)
             store_pair(i, i, 0)
-        for m in singles:
-            tile_pass("sq", 1, m, halves[0])
         for i in pairs:
             pair_pass("sq", 1, i, 1)
             pair_pass("lin", 1, i, 1, stop=True)

@@ -25,8 +25,6 @@ HALF = T // 2
 RUN = 4
 SHIFTS = 4
 SHIFT_COLS = M // SHIFTS
-EARLY = 8
-PAIRED = 6
 WARM_PASSES = 4
 TWO_ONES = 0x3F803F80
 ALIGN = 256
@@ -34,28 +32,23 @@ ALIGN = 256
 
 def tile_mix_feat_fm_quad_none_kernel(tc, x, w4_words, w4_scales, w8_words, w8_scales, out):
     nc = tc.nc
-    whole = slice(0, T)
-    halves = (slice(0, HALF), slice(HALF, T))
-    pairs = range(PAIRED // 2)
-    singles = range(PAIRED, EARLY)
-    pieces = [(m, whole) for m in range(EARLY, TILES - 2)]
-    pieces.extend([(TILES - 2, halves[0]), (TILES - 2, halves[1]), (TILES - 1, halves[0])])
-    pieces.extend([(TILES - 1, slice(HALF, HALF + P)), (TILES - 1, slice(HALF + P, T))])
 
     with ExitStack() as ctx:
         keep = ctx.enter_context(tc.tile_pool(name="keep", bufs=1))
-        stage = ctx.enter_context(tc.tile_pool(name="stage", bufs=2 * len(pairs) + len(pieces)))
         psum = ctx.enter_context(tc.psum_pool(name="psum", bufs=BANKS))
         ctx.enter_context(tc.manual_schedule())
 
-        s8 = keep.tile([P, PASSES * SHIFT_COLS], U8, name="s8", align_bytes=ALIGN)
-        s4 = keep.tile([P, PASSES * M], U8, name="s4", align_bytes=ALIGN)
-        ones = keep.tile([P, PACK * T // 4], BF16, name="ones", align_bytes=ALIGN)
+        def sbuf(name, shape, dtype):
+            return keep.tile(shape, dtype, name=name, align_bytes=ALIGN)
+
+        s8 = sbuf("s8", [P, PASSES * SHIFT_COLS], U8)
+        s4 = sbuf("s4", [P, PASSES * M], U8)
+        ones = sbuf("ones", [P, PACK * T // 4], BF16)
         nc.vector.memset(ones[:].bitcast(I32), TWO_ONES)
         nc.vector.memset(s8[:].bitcast(I32), 0)
 
-        warm_codes = keep.tile([P, T], U32, name="warm_codes", align_bytes=ALIGN)
-        warm_plane = keep.tile([P, T], U8, name="warm_plane", align_bytes=ALIGN)
+        warm_codes = sbuf("warm_codes", [P, T], U32)
+        warm_plane = sbuf("warm_plane", [P, T], U8)
         for lo in range(0, T, T // 4):
             cols = slice(lo, lo + T // 4)
             nc.vector.quantize_mx(out=warm_codes[:, cols].bitcast(FP8X4), scales=warm_plane[:, cols], in_=ones[:])
@@ -73,14 +66,26 @@ def tile_mix_feat_fm_quad_none_kernel(tc, x, w4_words, w4_scales, w8_words, w8_s
             )
 
         raw = {}
-        w8 = {}
-        w4 = {}
+        words = {}
 
         def load_x(a, h):
-            t = keep.tile([P, PACK, HALF], F32, name="raw_%d_%d" % (a, h), align_bytes=ALIGN)
+            raw[a, h] = sbuf("raw_%d_%d" % (a, h), [P, PACK, HALF], F32)
             rows = x[a * K_PASS : (a + 1) * K_PASS, h * HALF : (h + 1) * HALF]
+            nc.sync.dma_start(out=raw[a, h][:], in_=rows.rearrange("(p j) w -> p j w", j=PACK))
+
+        def load_x_columns(a, lo, hi):
+            t = sbuf("raw_%d_%d" % (a, lo), [P, PACK, hi - lo], F32)
+            rows = x[a * K_PASS : (a + 1) * K_PASS, lo:hi]
             nc.sync.dma_start(out=t[:], in_=rows.rearrange("(p j) w -> p j w", j=PACK))
-            raw[a, h] = t
+            for c in range(lo, hi, P):
+                raw[a, c] = t, lo
+
+        def load_x_pass(a):
+            both = sbuf("raw_%d" % a, [P, PACK, T], F32)
+            rows = x[a * K_PASS : (a + 1) * K_PASS, :]
+            nc.sync.dma_start(out=both[:], in_=rows.rearrange("(p j) w -> p j w", j=PACK))
+            for h in range(2):
+                raw[a, h] = both[:, :, h * HALF : (h + 1) * HALF]
 
         def load_w4_scales():
             for r in range(4):
@@ -94,86 +99,82 @@ def tile_mix_feat_fm_quad_none_kernel(tc, x, w4_words, w4_scales, w8_words, w8_s
                 src = w8_scales[a, 4 * q : 4 * q + 4, :].rearrange("r (c n) -> c r n", c=SHIFTS).bitcast(I32)
                 nc.sync.dma_start(out=dst, in_=src)
 
-        def load_words(name, words, views, word_bytes, passes, lo, hi):
-            width = (hi - lo) * P * word_bytes
-            t = keep.tile([P, len(passes) * width], U8, name="%s_%d_%d" % (name, passes[0], lo), align_bytes=ALIGN)
-            src = words[passes[0] : passes[-1] + 1, :, lo * P * word_bytes : hi * P * word_bytes]
+        def load_w(name, passes, pairs):
+            if name == "sq":
+                source, tile_bytes = w4_words, 2 * P
+            else:
+                source, tile_bytes = w8_words.rearrange("a p n i -> a p (n i)"), 4 * P
+            lo, hi = 2 * pairs[0], 2 * pairs[-1] + 2
+            width = (hi - lo) * tile_bytes
+            t = sbuf("w_%s_%d_%d" % (name, passes[0], lo), [P, len(passes) * width], U8)
+            src = source[passes[0] : passes[-1] + 1, :, lo * tile_bytes : hi * tile_bytes]
             nc.sync.dma_start(
                 out=t[:].bitcast(I32).rearrange("p (a n) -> p a n", a=len(passes)),
                 in_=src.rearrange("a p b -> p a b").bitcast(I32),
             )
             for i, a in enumerate(passes):
                 for m in range(lo, hi):
-                    first = i * width + (m - lo) * P * word_bytes
-                    views[a, m] = t[:, first : first + P * word_bytes]
+                    first = i * width + (m - lo) * tile_bytes
+                    words[name, a, m] = t[:, first : first + tile_bytes]
 
-        def load_w8(passes, lo, hi):
-            load_words("w8", w8_words.rearrange("a p n i -> a p (n i)"), w8, 4, passes, lo, hi)
-
-        def load_w4(passes, lo, hi):
-            load_words("w4", w4_words, w4, 2, passes, lo, hi)
-
-        load_x(0, 0)
+        load_x_columns(0, 0, HALF + P)
         load_w8_scales(0)
-        load_w8([0], 0, EARLY // 2)
-        load_x(0, 1)
-        load_w8([0], EARLY // 2, EARLY)
+        load_w("lin", [0], [0, 1])
+        load_x_columns(0, HALF + P, T)
+        load_w("lin", [0], [2, 3])
         load_w4_scales()
-        load_w4([0], 0, EARLY)
-        load_x(1, 0)
-        load_x(1, 1)
-        load_w4([1], 0, EARLY)
+        load_w("sq", [0], [0, 1])
+        load_x_columns(1, 0, HALF)
+        load_w("sq", [0], [2, 3])
+        load_w("sq", [1], [0, 1, 2, 3])
+        load_x_columns(1, HALF, T)
         load_w8_scales(1)
-        load_w8([1], 0, EARLY // 2)
-        load_w8([1], EARLY // 2, EARLY)
-        load_w8([0, 1], EARLY, TILES)
-        load_w4([0, 1], EARLY, TILES)
+        load_w("lin", [1], [0, 1])
+        load_w("lin", [1], [2, 3])
+        load_w("lin", [0, 1], [4, 5])
+        load_w("sq", [0, 1], [4, 5])
 
         codes = {}
         planes = {}
         for name in ("sq", "lin"):
             for a in range(PASSES):
-                codes[name, a] = keep.tile([P, T], U32, name="codes_%s_%d" % (name, a), align_bytes=ALIGN)
-                planes[name, a] = keep.tile([P, T], U8, name="plane_%s_%d" % (name, a), align_bytes=ALIGN)
+                codes[name, a] = sbuf("codes_%s_%d" % (name, a), [P, T], U32)
+                planes[name, a] = sbuf("plane_%s_%d" % (name, a), [P, T], U8)
 
         grouped = {}
 
-        def group(name, a, h, lo=0, hi=HALF, helper=False):
-            g = keep.tile([P, hi - lo, PACK], BF16, name="g_%s_%d_%d_%d" % (name, a, h, lo), align_bytes=ALIGN)
+        def group(engine, name, a, h, lo, hi):
+            g = sbuf("g_%s_%d_%d_%d" % (name, a, h, lo), [P, hi - lo, PACK], BF16)
             dst = g[:].rearrange("p (c i) j -> p c j i", i=RUN)
-            src = raw[a, h][:, :, lo:hi].rearrange("p j (c i) -> p c j i", i=RUN)
-            if name == "sq" and helper:
+            t, first = raw[a, h * HALF + lo]
+            src = t[:, :, h * HALF + lo - first : h * HALF + hi - first].rearrange("p j (c i) -> p c j i", i=RUN)
+            if engine == "vector" and name == "sq":
                 nc.vector.tensor_tensor(out=dst, in0=src, in1=src, op=MULT)
+            elif engine == "vector":
+                nc.vector.tensor_copy(out=dst, in_=src)
             elif name == "sq":
                 nc.scalar.activation(out=dst, in_=src, func=SQUARE)
-            elif helper:
-                nc.scalar.copy(out=dst, in_=src)
             else:
-                nc.vector.tensor_copy(out=dst, in_=src)
-            grouped[name, a, h, lo] = g
+                nc.scalar.copy(out=dst, in_=src)
+            grouped[name, a, h, lo] = g, hi
 
-        def quantize(name, a, h, lo=0, hi=HALF):
+        def quantize(name, a, h, lo):
+            g, hi = grouped[name, a, h, lo]
             cols = slice(h * HALF + lo, h * HALF + hi)
             nc.vector.quantize_mx(
                 out=codes[name, a][:, cols].bitcast(FP8X4),
                 scales=planes[name, a][:, cols],
-                in_=grouped[name, a, h, lo][:].rearrange("p w j -> p (w j)"),
+                in_=g[:].rearrange("p w j -> p (w j)"),
             )
 
-        def linear_operand(a, h):
-            for lo in (0, P):
-                group("lin", a, h, lo, lo + P)
-            for lo in (0, P):
-                quantize("lin", a, h, lo, lo + P)
-
-        def multiply(name, a, m, cols, dst, start=False, stop=False):
+        def multiply(name, a, m, cols, dst, start, stop):
             if name == "sq":
                 first = a * M + m * P
-                weights, weight_scales = w4[a, m].bitcast(FP4X4), s4[:, first : first + P]
+                weights, weight_scales = words[name, a, m].bitcast(FP4X4), s4[:, first : first + P]
             else:
                 c, offset = divmod(m * P, SHIFT_COLS)
                 first = a * SHIFT_COLS + offset
-                weights, weight_scales = w8[a, m].bitcast(FP8X4), s8[4 * c :, first : first + P]
+                weights, weight_scales = words[name, a, m].bitcast(FP8X4), s8[4 * c :, first : first + P]
             nc.tensor.matmul_mx(
                 out=dst,
                 lhsT=weights,
@@ -186,97 +187,125 @@ def tile_mix_feat_fm_quad_none_kernel(tc, x, w4_words, w4_scales, w8_words, w8_s
 
         acc = {}
 
-        def tile_pass(name, a, m, cols, start=False, stop=False):
-            if start:
-                acc[m] = psum.tile([P, T], F32, name="acc")
-            multiply(name, a, m, cols, acc[m][:, cols], start, stop)
-
         def pair_pass(name, a, i, h, start=False, stop=False, lo=0, hi=HALF):
             if start:
-                acc["pair", i, h] = psum.tile([P, T], F32, name="acc")
+                acc[i, h] = psum.tile([P, T], F32, name="acc")
             cols = slice(h * HALF + lo, h * HALF + hi)
             for u in range(2):
-                dst = acc["pair", i, h][:, u * HALF + lo : u * HALF + hi]
+                dst = acc[i, h][:, u * HALF + lo : u * HALF + hi]
                 multiply(name, a, 2 * i + u, cols, dst, start and u == 0, stop and u == 1)
 
-        def copy_out(turn, dst, src):
-            if turn % 2 == 0:
+        def copy_out(engine, dst, src):
+            if engine == "scalar":
                 nc.scalar.copy(out=dst, in_=src)
             else:
                 nc.vector.tensor_copy(out=dst, in_=src)
 
-        def store(turn, m, cols, sums):
-            width = cols.stop - cols.start
-            res = stage.tile([P, T], F32, name="res", align_bytes=ALIGN)
-            copy_out(turn, res[:, :width], sums)
-            nc.sync.dma_start(out=out[m * P : (m + 1) * P, cols], in_=res[:, :width])
+        def store(engine, first_tile, cols, res):
+            count = res.shape[1]
+            rows = out[first_tile * P : (first_tile + count) * P, cols].rearrange("(u p) c -> p u c", u=count)
+            nc.sync.dma_start(out=rows, in_=res)
 
-        def store_pair(turn, i, h):
-            res = stage.tile([P, T], F32, name="res", align_bytes=ALIGN)
-            copy_out(turn, res[:], acc["pair", i, h][:])
-            rows = out[2 * i * P : (2 * i + 2) * P, halves[h]].rearrange("(u p) c -> p u c", u=2)
-            nc.sync.dma_start(out=rows, in_=res[:].rearrange("p (u c) -> p u c", u=2))
+        def store_pair(engine, i, h):
+            res = sbuf("res_%d_%d" % (i, h), [P, 2, HALF], F32)
+            copy_out(engine, res[:].rearrange("p u c -> p (u c)"), acc[i, h][:])
+            store(engine, 2 * i, slice(h * HALF, (h + 1) * HALF), res[:])
 
-        group("sq", 0, 0)
-        linear_operand(0, 0)
-        quantize("sq", 0, 0)
-        group("lin", 0, 1, 0, P)
-        group("lin", 0, 1, P, HALF, helper=True)
-        group("sq", 0, 1)
+        staged = {}
+
+        def store_two(engine, i, h):
+            if i % 2 == 0:
+                staged[h] = sbuf("two_%d_%d" % (i, h), [P, 4, HALF], F32)
+            u = 2 * (i % 2)
+            copy_out(engine, staged[h][:, u : u + 2, :].rearrange("p u c -> p (u c)"), acc[i, h][:])
+            if i % 2:
+                store(engine, 2 * i - 2, slice(h * HALF, (h + 1) * HALF), staged[h][:])
+
+        def tile_pass(name, a, m, lo, hi, start=False, stop=False):
+            if start:
+                acc["t", m] = psum.tile([P, T], F32, name="acc")
+            multiply(name, a, m, slice(lo, hi), acc["t", m][:, lo:hi], start, stop)
+
+        def store_tile(engine, m):
+            res = sbuf("res_t_%d" % m, [P, 1, T], F32)
+            copy_out(engine, res[:, 0, :], acc["t", m][:])
+            store(engine, m, slice(0, T), res[:])
+
+        def piece(engine, m, lo, hi):
+            bank = psum.tile([P, T], F32, name="acc")
+            for a in range(PASSES):
+                multiply("lin", a, m, slice(lo, hi), bank[:, : hi - lo], a == 0, False)
+                multiply("sq", a, m, slice(lo, hi), bank[:, : hi - lo], False, a == PASSES - 1)
+            res = sbuf("res_%d_%d" % (m, lo), [P, 1, hi - lo], F32)
+            copy_out(engine, res[:, 0, :], bank[:, : hi - lo])
+            store(engine, m, slice(lo, hi), res[:])
+
+        group("scalar", "lin", 0, 1, 0, P)
+        group("scalar", "sq", 0, 0, 0, HALF)
+        group("vector", "lin", 0, 0, 0, P)
+        group("vector", "lin", 0, 0, P, HALF)
+        quantize("lin", 0, 0, 0)
+        quantize("lin", 0, 1, 0)
+        quantize("lin", 0, 0, P)
+        group("scalar", "sq", 0, 1, 0, P)
+        group("vector", "lin", 0, 1, P, HALF)
+        group("scalar", "sq", 0, 1, P, HALF)
+        quantize("lin", 0, 1, P)
+        quantize("sq", 0, 0, 0)
         for lo in (0, P):
-            quantize("lin", 0, 1, lo, lo + P)
-        quantize("sq", 0, 1)
-
+            quantize("sq", 0, 1, lo)
         for h in range(2):
-            group("sq", 1, h, 0, P)
-            group("sq", 1, h, P, HALF, helper=True)
-            group("lin", 1, h, 0, P)
-            group("lin", 1, h, P, HALF, helper=True)
+            group("scalar", "sq", 1, h, 0, P)
+            group("vector", "sq", 1, h, P, HALF)
+            group("vector", "lin", 1, h, 0, P)
+            group("scalar", "lin", 1, h, P, HALF)
             for lo in (P, 0):
-                quantize("sq", 1, h, lo, lo + P)
+                quantize("sq", 1, h, lo)
             for lo in (0, P):
-                quantize("lin", 1, h, lo, lo + P)
-
-        for lo in (0, P):
+                quantize("lin", 1, h, lo)
+        pairs = range(3)
+        singles = range(2 * 3, 8)
+        engines = ("scalar", "vector")
+        for h, lo in ((0, 0), (1, 0), (0, P)):
             for i in pairs[:2]:
-                pair_pass("lin", 0, i, 0, start=lo == 0, lo=lo, hi=lo + P)
+                pair_pass("lin", 0, i, h, start=lo == 0, lo=lo, hi=lo + P)
         for i in pairs[2:]:
             pair_pass("lin", 0, i, 0, start=True)
+            pair_pass("lin", 0, i, 1, start=True, hi=P)
         for m in singles:
-            tile_pass("lin", 0, m, halves[0], start=True)
+            tile_pass("lin", 0, m, 0, HALF, start=True)
+            tile_pass("lin", 0, m, HALF, HALF + P)
         for i in pairs:
-            pair_pass("lin", 0, i, 1, start=True)
+            pair_pass("lin", 0, i, 1, lo=P)
         for m in singles:
-            tile_pass("lin", 0, m, halves[1])
-        for h in range(2):
-            for i in pairs:
-                pair_pass("sq", 0, i, h)
+            tile_pass("lin", 0, m, HALF + P, T)
+        for some in (pairs[:2], pairs[2:]):
+            for h in range(2):
+                for i in some:
+                    pair_pass("sq", 0, i, h)
         for m in singles:
-            tile_pass("sq", 0, m, whole)
-
+            tile_pass("sq", 0, m, 0, T)
         for i in pairs:
             pair_pass("sq", 1, i, 0)
         for m in singles:
-            tile_pass("sq", 1, m, halves[0])
+            tile_pass("sq", 1, m, 0, HALF)
         for i in pairs:
             pair_pass("lin", 1, i, 0, stop=True)
-            store_pair(i, i, 0)
+            store_pair(engines[i % 2], i, 0)
         for i in pairs:
             pair_pass("sq", 1, i, 1)
             pair_pass("lin", 1, i, 1, stop=True)
-            store_pair(i, i, 1)
-        both = keep.tile([P, len(singles), T], F32, name="both", align_bytes=ALIGN)
+            store_pair(engines[i % 2], i, 1)
+        both = sbuf("both", [P, len(singles), T], F32)
         for m in singles:
-            tile_pass("sq", 1, m, halves[1])
-            tile_pass("lin", 1, m, whole, stop=True)
-            copy_out(m + 1, both[:, m - PAIRED, :], acc[m][:])
-        rows = out[PAIRED * P : EARLY * P, :].rearrange("(u p) c -> p u c", u=len(singles))
-        nc.sync.dma_start(out=rows, in_=both[:])
-
-        for turn, (m, cols) in enumerate(pieces):
-            bank = psum.tile([P, T], F32, name="acc")
-            sums = bank[:, : cols.stop - cols.start]
-            for a in range(PASSES):
-                multiply("lin", a, m, cols, sums, start=a == 0)
-                multiply("sq", a, m, cols, sums, stop=a == PASSES - 1)
-            store(turn, m, cols, sums)
+            tile_pass("sq", 1, m, HALF, T)
+            tile_pass("lin", 1, m, 0, T, stop=True)
+            copy_out(engines[(m + 1) % 2], both[:, m - 2 * 3, :], acc["t", m][:])
+        store("vector", 2 * 3, slice(0, T), both[:])
+        piece("scalar", 8, 0, T)
+        piece("vector", 9, 0, T)
+        piece("scalar", 10, 0, HALF)
+        piece("vector", 10, HALF, T)
+        piece("scalar", 11, 0, HALF)
+        piece("vector", 11, HALF, HALF + P)
+        piece("scalar", 11, HALF + P, T)

@@ -43,14 +43,14 @@ def tile_mix_feat_fm_quad_none_kernel(tc, x, w4_words, w4_scales, w8_words, w8_s
 
         s8 = sbuf("s8", [P, PASSES * SHIFT_COLS], U8)
         s4 = sbuf("s4", [P, PASSES * M], U8)
-        ones = sbuf("ones", [P, PACK * T // 4], BF16)
+        ones = sbuf("ones", [P, PACK * T // 2], BF16)
         nc.vector.memset(ones[:].bitcast(I32), TWO_ONES)
         nc.vector.memset(s8[:].bitcast(I32), 0)
 
         warm_codes = sbuf("warm_codes", [P, T], U32)
         warm_plane = sbuf("warm_plane", [P, T], U8)
-        for lo in range(0, T, T // 4):
-            cols = slice(lo, lo + T // 4)
+        for lo in range(0, T, T // 2):
+            cols = slice(lo, lo + T // 2)
             nc.vector.quantize_mx(out=warm_codes[:, cols].bitcast(FP8X4), scales=warm_plane[:, cols], in_=ones[:])
         nc.vector.memset(s4[:].bitcast(I32), 0)
         warm_bank = psum.tile([P, T], F32, name="acc")
@@ -99,12 +99,11 @@ def tile_mix_feat_fm_quad_none_kernel(tc, x, w4_words, w4_scales, w8_words, w8_s
                 src = w8_scales[a, 4 * q : 4 * q + 4, :].rearrange("r (c n) -> c r n", c=SHIFTS).bitcast(I32)
                 nc.sync.dma_start(out=dst, in_=src)
 
-        def load_w(name, passes, pairs):
+        def load_w(name, passes, lo, hi):
             if name == "sq":
                 source, tile_bytes = w4_words, 2 * P
             else:
                 source, tile_bytes = w8_words.rearrange("a p n i -> a p (n i)"), 4 * P
-            lo, hi = 2 * pairs[0], 2 * pairs[-1] + 2
             width = (hi - lo) * tile_bytes
             t = sbuf("w_%s_%d_%d" % (name, passes[0], lo), [P, len(passes) * width], U8)
             src = source[passes[0] : passes[-1] + 1, :, lo * tile_bytes : hi * tile_bytes]
@@ -119,20 +118,20 @@ def tile_mix_feat_fm_quad_none_kernel(tc, x, w4_words, w4_scales, w8_words, w8_s
 
         load_x_columns(0, 0, HALF + P)
         load_w8_scales(0)
-        load_w("lin", [0], [0, 1])
+        load_w("lin", [0], 0, 5)
         load_x_columns(0, HALF + P, T)
-        load_w("lin", [0], [2, 3])
+        load_w("lin", [0], 5, 8)
         load_w4_scales()
-        load_w("sq", [0], [0, 1])
+        load_w("sq", [0], 0, 4)
         load_x_columns(1, 0, HALF)
-        load_w("sq", [0], [2, 3])
-        load_w("sq", [1], [0, 1, 2, 3])
+        load_w("sq", [0], 4, 8)
+        load_w("sq", [1], 0, 8)
         load_x_columns(1, HALF, T)
         load_w8_scales(1)
-        load_w("lin", [1], [0, 1])
-        load_w("lin", [1], [2, 3])
-        load_w("lin", [0, 1], [4, 5])
-        load_w("sq", [0, 1], [4, 5])
+        load_w("lin", [1], 0, 4)
+        load_w("lin", [1], 4, 8)
+        load_w("lin", [0, 1], 8, 12)
+        load_w("sq", [0, 1], 8, 12)
 
         codes = {}
         planes = {}
@@ -144,9 +143,13 @@ def tile_mix_feat_fm_quad_none_kernel(tc, x, w4_words, w4_scales, w8_words, w8_s
         grouped = {}
 
         def group(engine, name, a, h, lo, hi):
-            g = sbuf("g_%s_%d_%d_%d" % (name, a, h, lo), [P, hi - lo, PACK], BF16)
-            dst = g[:].rearrange("p (c i) j -> p c j i", i=RUN)
-            t, first = raw[a, h * HALF + lo]
+            block = lo - lo % P
+            if (name, a, h, block) not in grouped:
+                width = max(P, hi - block)
+                g = sbuf("g_%s_%d_%d_%d" % (name, a, h, block), [P, width, PACK], BF16)
+                grouped[name, a, h, block] = g, block + width
+            dst = grouped[name, a, h, block][0][:, lo - block : hi - block, :].rearrange("p (c i) j -> p c j i", i=RUN)
+            t, first = raw[a, h * HALF + block]
             src = t[:, :, h * HALF + lo - first : h * HALF + hi - first].rearrange("p j (c i) -> p c j i", i=RUN)
             if engine == "vector" and name == "sq":
                 nc.vector.tensor_tensor(out=dst, in0=src, in1=src, op=MULT)
@@ -156,7 +159,6 @@ def tile_mix_feat_fm_quad_none_kernel(tc, x, w4_words, w4_scales, w8_words, w8_s
                 nc.scalar.activation(out=dst, in_=src, func=SQUARE)
             else:
                 nc.scalar.copy(out=dst, in_=src)
-            grouped[name, a, h, lo] = g, hi
 
         def quantize(name, a, h, lo):
             g, hi = grouped[name, a, h, lo]
@@ -187,11 +189,11 @@ def tile_mix_feat_fm_quad_none_kernel(tc, x, w4_words, w4_scales, w8_words, w8_s
 
         acc = {}
 
-        def pair_pass(name, a, i, h, start=False, stop=False, lo=0, hi=HALF):
+        def pair_pass(name, a, i, h, start=False, stop=False, lo=0, hi=HALF, tiles=(0, 1)):
             if start:
                 acc[i, h] = psum.tile([P, T], F32, name="acc")
             cols = slice(h * HALF + lo, h * HALF + hi)
-            for u in range(2):
+            for u in tiles:
                 dst = acc[i, h][:, u * HALF + lo : u * HALF + hi]
                 multiply(name, a, 2 * i + u, cols, dst, start and u == 0, stop and u == 1)
 
@@ -245,11 +247,11 @@ def tile_mix_feat_fm_quad_none_kernel(tc, x, w4_words, w4_scales, w8_words, w8_s
         group("vector", "lin", 0, 0, 0, P)
         group("vector", "lin", 0, 0, P, HALF)
         quantize("lin", 0, 0, 0)
-        quantize("lin", 0, 1, 0)
         quantize("lin", 0, 0, P)
+        quantize("lin", 0, 1, 0)
         group("scalar", "sq", 0, 1, 0, P)
         group("vector", "lin", 0, 1, P, HALF)
-        group("scalar", "sq", 0, 1, P, HALF)
+        group("vector", "sq", 0, 1, P, HALF)
         quantize("lin", 0, 1, P)
         quantize("sq", 0, 0, 0)
         for lo in (0, P):
@@ -258,7 +260,8 @@ def tile_mix_feat_fm_quad_none_kernel(tc, x, w4_words, w4_scales, w8_words, w8_s
             group("scalar", "sq", 1, h, 0, P)
             group("vector", "sq", 1, h, P, HALF)
             group("vector", "lin", 1, h, 0, P)
-            group("scalar", "lin", 1, h, P, HALF)
+            group("vector", "lin", 1, h, P, HALF - 96)
+            group("scalar", "lin", 1, h, HALF - 96, HALF)
             for lo in (P, 0):
                 quantize("sq", 1, h, lo)
             for lo in (0, P):
@@ -266,12 +269,14 @@ def tile_mix_feat_fm_quad_none_kernel(tc, x, w4_words, w4_scales, w8_words, w8_s
         pairs = range(3)
         singles = range(2 * 3, 8)
         engines = ("scalar", "vector")
-        for h, lo in ((0, 0), (1, 0), (0, P)):
+        for lo in (0, P):
             for i in pairs[:2]:
-                pair_pass("lin", 0, i, h, start=lo == 0, lo=lo, hi=lo + P)
-        for i in pairs[2:]:
-            pair_pass("lin", 0, i, 0, start=True)
+                pair_pass("lin", 0, i, 0, start=lo == 0, lo=lo, hi=lo + P)
+        for i in pairs[:2]:
             pair_pass("lin", 0, i, 1, start=True, hi=P)
+        for u in range(2):
+            pair_pass("lin", 0, 2, 0, start=u == 0, tiles=(u,))
+            pair_pass("lin", 0, 2, 1, start=u == 0, hi=P, tiles=(u,))
         for m in singles:
             tile_pass("lin", 0, m, 0, HALF, start=True)
             tile_pass("lin", 0, m, HALF, HALF + P)

@@ -25,6 +25,11 @@ HALF = T // 2
 RUN = 4
 SHIFTS = 4
 SHIFT_COLS = M // SHIFTS
+EARLY = BANKS
+PAIRS = 3
+FIRST = 5
+EARLY_COLS = EARLY * P
+SCALAR_COLS = 96
 WARM_PASSES = 4
 TWO_ONES = 0x3F803F80
 ALIGN = 256
@@ -42,7 +47,8 @@ def tile_mix_feat_fm_quad_none_kernel(tc, x, w4_words, w4_scales, w8_words, w8_s
             return keep.tile(shape, dtype, name=name, align_bytes=ALIGN)
 
         s8 = sbuf("s8", [P, PASSES * SHIFT_COLS], U8)
-        s4 = sbuf("s4", [P, PASSES * M], U8)
+        s4 = sbuf("s4", [P, PASSES * EARLY_COLS], U8)
+        s4_late = sbuf("s4_late", [P, PASSES * (M - EARLY_COLS)], U8)
         ones = sbuf("ones", [P, PACK * T // 2], BF16)
         nc.vector.memset(ones[:].bitcast(I32), TWO_ONES)
         nc.vector.memset(s8[:].bitcast(I32), 0)
@@ -53,6 +59,7 @@ def tile_mix_feat_fm_quad_none_kernel(tc, x, w4_words, w4_scales, w8_words, w8_s
             cols = slice(lo, lo + T // 2)
             nc.vector.quantize_mx(out=warm_codes[:, cols].bitcast(FP8X4), scales=warm_plane[:, cols], in_=ones[:])
         nc.vector.memset(s4[:].bitcast(I32), 0)
+        nc.vector.memset(s4_late[:].bitcast(I32), 0)
         warm_bank = psum.tile([P, T], F32, name="acc")
         for i in range(WARM_PASSES):
             nc.tensor.matmul_mx(
@@ -68,29 +75,17 @@ def tile_mix_feat_fm_quad_none_kernel(tc, x, w4_words, w4_scales, w8_words, w8_s
         raw = {}
         words = {}
 
-        def load_x(a, h):
-            raw[a, h] = sbuf("raw_%d_%d" % (a, h), [P, PACK, HALF], F32)
-            rows = x[a * K_PASS : (a + 1) * K_PASS, h * HALF : (h + 1) * HALF]
-            nc.sync.dma_start(out=raw[a, h][:], in_=rows.rearrange("(p j) w -> p j w", j=PACK))
-
-        def load_x_columns(a, lo, hi):
+        def load_x(a, lo, hi):
             t = sbuf("raw_%d_%d" % (a, lo), [P, PACK, hi - lo], F32)
             rows = x[a * K_PASS : (a + 1) * K_PASS, lo:hi]
             nc.sync.dma_start(out=t[:], in_=rows.rearrange("(p j) w -> p j w", j=PACK))
             for c in range(lo, hi, P):
                 raw[a, c] = t, lo
 
-        def load_x_pass(a):
-            both = sbuf("raw_%d" % a, [P, PACK, T], F32)
-            rows = x[a * K_PASS : (a + 1) * K_PASS, :]
-            nc.sync.dma_start(out=both[:], in_=rows.rearrange("(p j) w -> p j w", j=PACK))
-            for h in range(2):
-                raw[a, h] = both[:, :, h * HALF : (h + 1) * HALF]
-
-        def load_w4_scales():
+        def load_w4_scales(plane, lo, hi):
             for r in range(4):
-                dst = s4[r:P:32, :].rearrange("q (a n) -> q a n", a=PASSES)
-                src = w4_scales[:, r:16:4, :].rearrange("a q n -> q a n")
+                dst = plane[r:P:32, :].rearrange("q (a n) -> q a n", a=PASSES)
+                src = w4_scales[:, r:16:4, lo:hi].rearrange("a q n -> q a n")
                 nc.sync.dma_start(out=dst.bitcast(I32), in_=src.bitcast(I32))
 
         def load_w8_scales(a):
@@ -116,22 +111,22 @@ def tile_mix_feat_fm_quad_none_kernel(tc, x, w4_words, w4_scales, w8_words, w8_s
                     first = i * width + (m - lo) * tile_bytes
                     words[name, a, m] = t[:, first : first + tile_bytes]
 
-        load_x_columns(0, 0, HALF + P)
+        load_x(0, 0, HALF + P)
         load_w8_scales(0)
-        load_w("lin", [0], 0, 5)
-        load_x_columns(0, HALF + P, T)
-        load_w("lin", [0], 5, 8)
-        load_w4_scales()
-        load_w("sq", [0], 0, 4)
-        load_x_columns(1, 0, HALF)
-        load_w("sq", [0], 4, 8)
-        load_w("sq", [1], 0, 8)
-        load_x_columns(1, HALF, T)
+        load_w("lin", [0], 0, FIRST)
+        load_x(0, HALF + P, T)
+        load_w("lin", [0], FIRST, EARLY)
+        load_w4_scales(s4, 0, EARLY_COLS)
+        load_w("sq", [0], 0, EARLY)
+        load_x(1, 0, HALF)
+        load_w("sq", [1], 0, EARLY)
+        load_x(1, HALF, T)
         load_w8_scales(1)
-        load_w("lin", [1], 0, 4)
-        load_w("lin", [1], 4, 8)
-        load_w("lin", [0, 1], 8, 12)
-        load_w("sq", [0, 1], 8, 12)
+        load_w("lin", [1], 0, EARLY // 2)
+        load_w("lin", [1], EARLY // 2, EARLY)
+        load_w("lin", [0, 1], EARLY, TILES)
+        load_w4_scales(s4_late, EARLY_COLS, M)
+        load_w("sq", [0, 1], EARLY, TILES)
 
         codes = {}
         planes = {}
@@ -171,8 +166,11 @@ def tile_mix_feat_fm_quad_none_kernel(tc, x, w4_words, w4_scales, w8_words, w8_s
 
         def multiply(name, a, m, cols, dst, start, stop):
             if name == "sq":
-                first = a * M + m * P
-                weights, weight_scales = words[name, a, m].bitcast(FP4X4), s4[:, first : first + P]
+                if m * P < EARLY_COLS:
+                    plane, first = s4, a * EARLY_COLS + m * P
+                else:
+                    plane, first = s4_late, a * (M - EARLY_COLS) + m * P - EARLY_COLS
+                weights, weight_scales = words[name, a, m].bitcast(FP4X4), plane[:, first : first + P]
             else:
                 c, offset = divmod(m * P, SHIFT_COLS)
                 first = a * SHIFT_COLS + offset
@@ -203,35 +201,26 @@ def tile_mix_feat_fm_quad_none_kernel(tc, x, w4_words, w4_scales, w8_words, w8_s
             else:
                 nc.vector.tensor_copy(out=dst, in_=src)
 
-        def store(engine, first_tile, cols, res):
+        def store(first_tile, cols, res):
             count = res.shape[1]
             rows = out[first_tile * P : (first_tile + count) * P, cols].rearrange("(u p) c -> p u c", u=count)
             nc.sync.dma_start(out=rows, in_=res)
 
-        def store_pair(engine, i, h):
-            res = sbuf("res_%d_%d" % (i, h), [P, 2, HALF], F32)
-            copy_out(engine, res[:].rearrange("p u c -> p (u c)"), acc[i, h][:])
-            store(engine, 2 * i, slice(h * HALF, (h + 1) * HALF), res[:])
-
         staged = {}
 
-        def store_two(engine, i, h):
-            if i % 2 == 0:
-                staged[h] = sbuf("two_%d_%d" % (i, h), [P, 4, HALF], F32)
-            u = 2 * (i % 2)
-            copy_out(engine, staged[h][:, u : u + 2, :].rearrange("p u c -> p (u c)"), acc[i, h][:])
-            if i % 2:
-                store(engine, 2 * i - 2, slice(h * HALF, (h + 1) * HALF), staged[h][:])
+        def empty_pair(engine, i, h):
+            if i < 2:
+                staged[h] = sbuf("res_%d_%d" % (i, h), [P, 2 + 2 * i, HALF], F32), i
+            res, first = staged[h]
+            u = 2 * (i - first)
+            copy_out(engine, res[:, u : u + 2, :].rearrange("p u c -> p (u c)"), acc[i, h][:])
+            if i != 1:
+                store(2 * first, slice(h * HALF, (h + 1) * HALF), res[:])
 
         def tile_pass(name, a, m, lo, hi, start=False, stop=False):
             if start:
                 acc["t", m] = psum.tile([P, T], F32, name="acc")
             multiply(name, a, m, slice(lo, hi), acc["t", m][:, lo:hi], start, stop)
-
-        def store_tile(engine, m):
-            res = sbuf("res_t_%d" % m, [P, 1, T], F32)
-            copy_out(engine, res[:, 0, :], acc["t", m][:])
-            store(engine, m, slice(0, T), res[:])
 
         def piece(engine, m, lo, hi):
             bank = psum.tile([P, T], F32, name="acc")
@@ -240,35 +229,36 @@ def tile_mix_feat_fm_quad_none_kernel(tc, x, w4_words, w4_scales, w8_words, w8_s
                 multiply("sq", a, m, slice(lo, hi), bank[:, : hi - lo], False, a == PASSES - 1)
             res = sbuf("res_%d_%d" % (m, lo), [P, 1, hi - lo], F32)
             copy_out(engine, res[:, 0, :], bank[:, : hi - lo])
-            store(engine, m, slice(lo, hi), res[:])
+            store(m, slice(lo, hi), res[:])
+
+        pairs = range(PAIRS)
+        singles = range(2 * PAIRS, EARLY)
+        engines = ("scalar", "vector")
 
         group("scalar", "lin", 0, 1, 0, P)
         group("scalar", "sq", 0, 0, 0, HALF)
-        group("vector", "lin", 0, 0, 0, P)
-        group("vector", "lin", 0, 0, P, HALF)
-        quantize("lin", 0, 0, 0)
-        quantize("lin", 0, 0, P)
-        quantize("lin", 0, 1, 0)
+        for lo in (0, P):
+            group("vector", "lin", 0, 0, lo, lo + P)
+        for h, lo in ((0, 0), (0, P), (1, 0)):
+            quantize("lin", 0, h, lo)
         group("scalar", "sq", 0, 1, 0, P)
         group("vector", "lin", 0, 1, P, HALF)
-        group("vector", "sq", 0, 1, P, HALF)
         quantize("lin", 0, 1, P)
-        quantize("sq", 0, 0, 0)
-        for lo in (0, P):
-            quantize("sq", 0, 1, lo)
+        group("vector", "sq", 0, 1, P, HALF)
+        for h, lo in ((0, 0), (1, 0), (1, P)):
+            quantize("sq", 0, h, lo)
+
         for h in range(2):
             group("scalar", "sq", 1, h, 0, P)
             group("vector", "sq", 1, h, P, HALF)
             group("vector", "lin", 1, h, 0, P)
-            group("vector", "lin", 1, h, P, HALF - 96)
-            group("scalar", "lin", 1, h, HALF - 96, HALF)
+            group("vector", "lin", 1, h, P, HALF - SCALAR_COLS)
+            group("scalar", "lin", 1, h, HALF - SCALAR_COLS, HALF)
             for lo in (P, 0):
                 quantize("sq", 1, h, lo)
             for lo in (0, P):
                 quantize("lin", 1, h, lo)
-        pairs = range(3)
-        singles = range(2 * 3, 8)
-        engines = ("scalar", "vector")
+
         for lo in (0, P):
             for i in pairs[:2]:
                 pair_pass("lin", 0, i, 0, start=lo == 0, lo=lo, hi=lo + P)
@@ -284,33 +274,33 @@ def tile_mix_feat_fm_quad_none_kernel(tc, x, w4_words, w4_scales, w8_words, w8_s
             pair_pass("lin", 0, i, 1, lo=P)
         for m in singles:
             tile_pass("lin", 0, m, HALF + P, T)
-        for some in (pairs[:2], pairs[2:]):
-            for h in range(2):
-                for i in some:
-                    pair_pass("sq", 0, i, h)
+
+        for h in range(2):
+            for i in pairs:
+                pair_pass("sq", 0, i, h)
         for m in singles:
             tile_pass("sq", 0, m, 0, T)
+
         for i in pairs:
             pair_pass("sq", 1, i, 0)
         for m in singles:
             tile_pass("sq", 1, m, 0, HALF)
         for i in pairs:
             pair_pass("lin", 1, i, 0, stop=True)
-            store_pair(engines[i % 2], i, 0)
+            empty_pair(engines[i % 2], i, 0)
         for i in pairs:
             pair_pass("sq", 1, i, 1)
             pair_pass("lin", 1, i, 1, stop=True)
-            store_pair(engines[i % 2], i, 1)
+            empty_pair(engines[i % 2], i, 1)
         both = sbuf("both", [P, len(singles), T], F32)
-        for m in singles:
+        for u, m in enumerate(singles):
             tile_pass("sq", 1, m, HALF, T)
             tile_pass("lin", 1, m, 0, T, stop=True)
-            copy_out(engines[(m + 1) % 2], both[:, m - 2 * 3, :], acc["t", m][:])
-        store("vector", 2 * 3, slice(0, T), both[:])
-        piece("scalar", 8, 0, T)
-        piece("vector", 9, 0, T)
-        piece("scalar", 10, 0, HALF)
-        piece("vector", 10, HALF, T)
-        piece("scalar", 11, 0, HALF)
-        piece("vector", 11, HALF, HALF + P)
-        piece("scalar", 11, HALF + P, T)
+            copy_out(engines[1 - u], both[:, u, :], acc["t", m][:])
+        store(singles[0], slice(0, T), both[:])
+
+        pieces = [(m, 0, T) for m in range(EARLY, TILES - 2)]
+        pieces.extend([(TILES - 2, 0, HALF), (TILES - 2, HALF, T), (TILES - 1, 0, HALF)])
+        pieces.extend([(TILES - 1, HALF, HALF + P), (TILES - 1, HALF + P, T)])
+        for turn, (m, lo, hi) in enumerate(pieces):
+            piece(engines[turn % 2], m, lo, hi)

from contextlib import ExitStack

import concourse.mybir as mybir

K, M, T = 1024, 1536, 512
FLOPS = 2 * 2 * K * M * T

F32 = mybir.dt.float32
BF16 = mybir.dt.bfloat16
I32 = mybir.dt.int32
U32 = mybir.dt.uint32
U8 = mybir.dt.uint8
FP8X4 = mybir.dt.float8_e4m3fn_x4
FP4X4 = mybir.dt.float4_e2m1fn_x4
SQUARE = mybir.ActivationFunctionType.Square
MULT = mybir.AluOpType.mult

P = 128
PACK = 4
K_PASS = P * PACK
PASSES = K // K_PASS
TILES = M // P
BANKS = 8
HALF = T // 2
RUN = 4
SHIFTS = 4
SHIFT_COLS = M // SHIFTS
EARLY = BANKS
PAIRS = 3
FIRST = 5
EARLY_COLS = EARLY * P
SCALAR_COLS = 96
WARM_PASSES = 4
TWO_ONES = 0x3F803F80
ALIGN = 256


def tile_mix_feat_fm_quad_none_kernel(tc, x, w4_words, w4_scales, w8_words, w8_scales, out):
    nc = tc.nc

    with ExitStack() as ctx:
        keep = ctx.enter_context(tc.tile_pool(name="keep", bufs=1))
        psum = ctx.enter_context(tc.psum_pool(name="psum", bufs=BANKS))
        ctx.enter_context(tc.manual_schedule())

        def sbuf(name, shape, dtype):
            return keep.tile(shape, dtype, name=name, align_bytes=ALIGN)

        s8 = sbuf("s8", [P, PASSES * SHIFT_COLS], U8)
        s4 = sbuf("s4", [P, PASSES * EARLY_COLS], U8)
        s4_late = sbuf("s4_late", [P, PASSES * (M - EARLY_COLS)], U8)
        ones = sbuf("ones", [P, PACK * T // 2], BF16)
        nc.vector.memset(ones[:].bitcast(I32), TWO_ONES)
        nc.vector.memset(s8[:].bitcast(I32), 0)

        warm_codes = sbuf("warm_codes", [P, T], U32)
        warm_plane = sbuf("warm_plane", [P, T], U8)
        for lo in range(0, T, T // 2):
            cols = slice(lo, lo + T // 2)
            nc.vector.quantize_mx(out=warm_codes[:, cols].bitcast(FP8X4), scales=warm_plane[:, cols], in_=ones[:])
        nc.vector.memset(s4[:].bitcast(I32), 0)
        nc.vector.memset(s4_late[:].bitcast(I32), 0)
        warm_bank = psum.tile([P, T], F32, name="acc")
        for i in range(WARM_PASSES):
            nc.tensor.matmul_mx(
                out=warm_bank[:],
                lhsT=warm_codes[:, :P].bitcast(FP8X4),
                lhsT_scale=warm_plane[:, :P],
                rhs=warm_codes[:].bitcast(FP8X4),
                rhs_scale=warm_plane[:],
                start=True,
                stop=True,
            )

        raw = {}
        words = {}

        def load_x(a, lo, hi):
            t = sbuf("raw_%d_%d" % (a, lo), [P, PACK, hi - lo], F32)
            rows = x[a * K_PASS : (a + 1) * K_PASS, lo:hi]
            nc.sync.dma_start(out=t[:], in_=rows.rearrange("(p j) w -> p j w", j=PACK))
            for c in range(lo, hi, P):
                raw[a, c] = t, lo

        def load_w4_scales(plane, lo, hi):
            for r in range(4):
                dst = plane[r:P:32, :].rearrange("q (a n) -> q a n", a=PASSES)
                src = w4_scales[:, r:16:4, lo:hi].rearrange("a q n -> q a n")
                nc.sync.dma_start(out=dst.bitcast(I32), in_=src.bitcast(I32))

        def load_w8_scales(a):
            for q in range(4):
                dst = s8[32 * q : 32 * q + 16, a * SHIFT_COLS : (a + 1) * SHIFT_COLS].bitcast(I32)
                src = w8_scales[a, 4 * q : 4 * q + 4, :].rearrange("r (c n) -> c r n", c=SHIFTS).bitcast(I32)
                nc.sync.dma_start(out=dst, in_=src)

        def load_w(name, passes, lo, hi):
            if name == "sq":
                source, tile_bytes = w4_words, 2 * P
            else:
                source, tile_bytes = w8_words.rearrange("a p n i -> a p (n i)"), 4 * P
            width = (hi - lo) * tile_bytes
            t = sbuf("w_%s_%d_%d" % (name, passes[0], lo), [P, len(passes) * width], U8)
            src = source[passes[0] : passes[-1] + 1, :, lo * tile_bytes : hi * tile_bytes]
            nc.sync.dma_start(
                out=t[:].bitcast(I32).rearrange("p (a n) -> p a n", a=len(passes)),
                in_=src.rearrange("a p b -> p a b").bitcast(I32),
            )
            for i, a in enumerate(passes):
                for m in range(lo, hi):
                    first = i * width + (m - lo) * tile_bytes
                    words[name, a, m] = t[:, first : first + tile_bytes]

        load_x(0, 0, HALF + P)
        load_w8_scales(0)
        load_w("lin", [0], 0, FIRST)
        load_x(0, HALF + P, T)
        load_w("lin", [0], FIRST, EARLY)
        load_w4_scales(s4, 0, EARLY_COLS)
        load_w("sq", [0], 0, EARLY)
        load_x(1, 0, HALF)
        load_w("sq", [1], 0, EARLY)
        load_x(1, HALF, T)
        load_w8_scales(1)
        load_w("lin", [1], 0, EARLY // 2)
        load_w("lin", [1], EARLY // 2, EARLY)
        load_w("lin", [0, 1], EARLY, TILES)
        load_w4_scales(s4_late, EARLY_COLS, M)
        load_w("sq", [0, 1], EARLY, TILES)

        codes = {}
        planes = {}
        for name in ("sq", "lin"):
            for a in range(PASSES):
                codes[name, a] = sbuf("codes_%s_%d" % (name, a), [P, T], U32)
                planes[name, a] = sbuf("plane_%s_%d" % (name, a), [P, T], U8)

        grouped = {}

        def group(engine, name, a, h, lo, hi):
            block = lo - lo % P
            if (name, a, h, block) not in grouped:
                width = max(P, hi - block)
                g = sbuf("g_%s_%d_%d_%d" % (name, a, h, block), [P, width, PACK], BF16)
                grouped[name, a, h, block] = g, block + width
            dst = grouped[name, a, h, block][0][:, lo - block : hi - block, :].rearrange("p (c i) j -> p c j i", i=RUN)
            t, first = raw[a, h * HALF + block]
            src = t[:, :, h * HALF + lo - first : h * HALF + hi - first].rearrange("p j (c i) -> p c j i", i=RUN)
            if engine == "vector" and name == "sq":
                nc.vector.tensor_tensor(out=dst, in0=src, in1=src, op=MULT)
            elif engine == "vector":
                nc.vector.tensor_copy(out=dst, in_=src)
            elif name == "sq":
                nc.scalar.activation(out=dst, in_=src, func=SQUARE)
            else:
                nc.scalar.copy(out=dst, in_=src)

        def quantize(name, a, h, lo):
            g, hi = grouped[name, a, h, lo]
            cols = slice(h * HALF + lo, h * HALF + hi)
            nc.vector.quantize_mx(
                out=codes[name, a][:, cols].bitcast(FP8X4),
                scales=planes[name, a][:, cols],
                in_=g[:].rearrange("p w j -> p (w j)"),
            )

        def multiply(name, a, m, cols, dst, start, stop):
            if name == "sq":
                if m * P < EARLY_COLS:
                    plane, first = s4, a * EARLY_COLS + m * P
                else:
                    plane, first = s4_late, a * (M - EARLY_COLS) + m * P - EARLY_COLS
                weights, weight_scales = words[name, a, m].bitcast(FP4X4), plane[:, first : first + P]
            else:
                c, offset = divmod(m * P, SHIFT_COLS)
                first = a * SHIFT_COLS + offset
                weights, weight_scales = words[name, a, m].bitcast(FP8X4), s8[4 * c :, first : first + P]
            nc.tensor.matmul_mx(
                out=dst,
                lhsT=weights,
                lhsT_scale=weight_scales,
                rhs=codes[name, a][:, cols].bitcast(FP8X4),
                rhs_scale=planes[name, a][:, cols],
                start=start,
                stop=stop,
            )

        acc = {}

        def pair_pass(name, a, i, h, start=False, stop=False, lo=0, hi=HALF, tiles=(0, 1)):
            if start:
                acc[i, h] = psum.tile([P, T], F32, name="acc")
            cols = slice(h * HALF + lo, h * HALF + hi)
            for u in tiles:
                dst = acc[i, h][:, u * HALF + lo : u * HALF + hi]
                multiply(name, a, 2 * i + u, cols, dst, start and u == 0, stop and u == 1)

        def copy_out(engine, dst, src):
            if engine == "scalar":
                nc.scalar.copy(out=dst, in_=src)
            else:
                nc.vector.tensor_copy(out=dst, in_=src)

        def store(first_tile, cols, res):
            count = res.shape[1]
            rows = out[first_tile * P : (first_tile + count) * P, cols].rearrange("(u p) c -> p u c", u=count)
            nc.sync.dma_start(out=rows, in_=res)

        staged = {}

        def empty_pair(engine, i, h):
            if i < 2:
                staged[h] = sbuf("res_%d_%d" % (i, h), [P, 2 + 2 * i, HALF], F32), i
            res, first = staged[h]
            u = 2 * (i - first)
            copy_out(engine, res[:, u : u + 2, :].rearrange("p u c -> p (u c)"), acc[i, h][:])
            if i != 1:
                store(2 * first, slice(h * HALF, (h + 1) * HALF), res[:])

        def tile_pass(name, a, m, lo, hi, start=False, stop=False):
            if start:
                acc["t", m] = psum.tile([P, T], F32, name="acc")
            multiply(name, a, m, slice(lo, hi), acc["t", m][:, lo:hi], start, stop)

        def piece(engine, m, lo, hi):
            bank = psum.tile([P, T], F32, name="acc")
            for a in range(PASSES):
                multiply("lin", a, m, slice(lo, hi), bank[:, : hi - lo], a == 0, False)
                multiply("sq", a, m, slice(lo, hi), bank[:, : hi - lo], False, a == PASSES - 1)
            res = sbuf("res_%d_%d" % (m, lo), [P, 1, hi - lo], F32)
            copy_out(engine, res[:, 0, :], bank[:, : hi - lo])
            store(m, slice(lo, hi), res[:])

        pairs = range(PAIRS)
        singles = range(2 * PAIRS, EARLY)
        engines = ("scalar", "vector")

        group("scalar", "lin", 0, 1, 0, P)
        group("scalar", "sq", 0, 0, 0, HALF)
        for lo in (0, P):
            group("vector", "lin", 0, 0, lo, lo + P)
        for h, lo in ((0, 0), (0, P), (1, 0)):
            quantize("lin", 0, h, lo)
        group("scalar", "sq", 0, 1, 0, P)
        group("vector", "lin", 0, 1, P, HALF)
        quantize("lin", 0, 1, P)
        group("vector", "sq", 0, 1, P, HALF)
        for h, lo in ((0, 0), (1, 0), (1, P)):
            quantize("sq", 0, h, lo)

        for h in range(2):
            group("scalar", "sq", 1, h, 0, P)
            group("vector", "sq", 1, h, P, HALF)
            group("vector", "lin", 1, h, 0, P)
            group("vector", "lin", 1, h, P, HALF - SCALAR_COLS)
            group("scalar", "lin", 1, h, HALF - SCALAR_COLS, HALF)
            for lo in (P, 0):
                quantize("sq", 1, h, lo)
            for lo in (0, P):
                quantize("lin", 1, h, lo)

        for lo in (0, P):
            for i in pairs[:2]:
                pair_pass("lin", 0, i, 0, start=lo == 0, lo=lo, hi=lo + P)
        for i in pairs[:2]:
            pair_pass("lin", 0, i, 1, start=True, hi=P)
        for u in range(2):
            pair_pass("lin", 0, 2, 0, start=u == 0, tiles=(u,))
            pair_pass("lin", 0, 2, 1, start=u == 0, hi=P, tiles=(u,))
        for m in singles:
            tile_pass("lin", 0, m, 0, HALF, start=True)
            tile_pass("lin", 0, m, HALF, HALF + P)
        for i in pairs:
            pair_pass("lin", 0, i, 1, lo=P)
        for m in singles:
            tile_pass("lin", 0, m, HALF + P, T)

        for h in range(2):
            for i in pairs:
                pair_pass("sq", 0, i, h)
        for m in singles:
            tile_pass("sq", 0, m, 0, T)

        for i in pairs:
            pair_pass("sq", 1, i, 0)
        for m in singles:
            tile_pass("sq", 1, m, 0, HALF)
        for i in pairs:
            pair_pass("lin", 1, i, 0, stop=True)
            empty_pair(engines[i % 2], i, 0)
        for i in pairs:
            pair_pass("sq", 1, i, 1)
            pair_pass("lin", 1, i, 1, stop=True)
            empty_pair(engines[i % 2], i, 1)
        both = sbuf("both", [P, len(singles), T], F32)
        for u, m in enumerate(singles):
            tile_pass("sq", 1, m, HALF, T)
            tile_pass("lin", 1, m, 0, T, stop=True)
            copy_out(engines[1 - u], both[:, u, :], acc["t", m][:])
        store(singles[0], slice(0, T), both[:])

        pieces = [(m, 0, T) for m in range(EARLY, TILES - 2)]
        pieces.extend([(TILES - 2, 0, HALF), (TILES - 2, HALF, T), (TILES - 1, 0, HALF)])
        pieces.extend([(TILES - 1, HALF, HALF + P), (TILES - 1, HALF + P, T)])
        for turn, (m, lo, hi) in enumerate(pieces):
            piece(engines[turn % 2], m, lo, hi)
